import numpy as np
import ml_dtypes


def mxq(x, axis, fmt="e4m3"):
    dtype, down = {"e4m3": (ml_dtypes.float8_e4m3fn, 7), "e5m2": (ml_dtypes.float8_e5m2, 14)}[fmt]
    v = np.moveaxis(np.asarray(x, np.float32).astype(ml_dtypes.bfloat16).astype(np.float64), axis, -1)
    blocks = v.reshape(v.shape[:-1] + (-1, 32))
    amax = np.abs(blocks).max(-1, keepdims=True)
    byte = np.maximum(np.where(amax > 0, np.frexp(amax)[1] - 1 + 127, 0) - down, 1)
    scale = np.exp2(byte - 127.0)
    codes = (blocks / scale).astype(np.float32).astype(dtype).astype(np.float64)
    return np.moveaxis((codes * scale).reshape(v.shape), -1, axis)


WIDE = False


def mx_kscale(k):
    if not WIDE:
        return np.ones(k)
    levels = np.array([10, -10, 5, -5, 0])
    if k % 512:
        return np.exp2(np.random.permutation(np.resize(levels, k // 32))).repeat(32)
    a = np.empty((k // 512, 16))
    for p in range(k // 512):
        a[p, :8] = np.random.permutation(np.resize(levels, 8))
        for g in range(8):
            far = levels[np.abs(levels - a[p, g]) >= 10]
            a[p, g + 8] = far[np.random.randint(len(far))]
    return np.exp2(a.ravel()).repeat(32)


BF16 = ml_dtypes.bfloat16


def bf(x):
    return np.asarray(x, np.float32).astype(BF16)


def f64(x):
    return np.asarray(x).astype(np.float64)


E2M1 = np.array([0.0, 0.5, 1.0, 1.5, 2.0, 3.0, 4.0, 6.0, -0.0, -0.5, -1.0, -1.5, -2.0, -3.0, -4.0, -6.0])


def pack_weight(w, fmt):
    k, n = w.shape
    w = f64(bf(w)).reshape(k // 32, 32, n)
    amax = np.abs(w).max(1)
    if fmt == "e4m3":
        byte = np.frexp(amax)[1] - 1 + 127 - 7
    else:
        mant, ex = np.frexp(amax / 6.0)
        byte = np.where(mant > 0.5, ex, ex - 1) + 127
    byte = np.clip(np.where(amax > 0, byte, 1), 1, 254)
    scaled = (w * np.exp2(127.0 - byte)[:, None, :]).reshape(k, n).astype(np.float32)
    by_word = np.ascontiguousarray(scaled.reshape(k // 512, 128, 4, n).transpose(0, 1, 3, 2))
    if fmt == "e4m3":
        words = by_word.astype(ml_dtypes.float8_e4m3fn).view(np.uint8)
    else:
        c = by_word.astype(ml_dtypes.float4_e2m1fn).view(np.uint8) & 0xF
        words = c[..., 0::2] | (c[..., 1::2] << 4)
    return np.ascontiguousarray(words), np.ascontiguousarray(byte.astype(np.uint8).reshape(k // 512, 16, n))


def unpack_weight(words, scales, fmt):
    g, p, n, _ = words.shape
    if fmt == "e4m3":
        vals = np.ascontiguousarray(words).view(ml_dtypes.float8_e4m3fn).astype(np.float64)
    else:
        nib = np.empty((g, p, n, 4), np.uint8)
        nib[..., 0::2] = words & 0xF
        nib[..., 1::2] = words >> 4
        vals = E2M1[nib]
    vals = vals * np.repeat(np.exp2(scales.astype(np.float64) - 127.0), 8, axis=1)[..., None]
    return vals.transpose(0, 1, 3, 2).reshape(g * 512, n)
def pack4(w):
    words, scales = pack_weight(w, "e2m1")
    return words.reshape(words.shape[0], 128, -1), scales


def unpack4(words, scales):
    return unpack_weight(words.reshape(words.shape[0], 128, -1, 2), scales, "e2m1")


def planes(Y):
    n, m = Y.shape
    b = f64(bf(Y)).reshape(n // 32, 32, m)
    amax = np.abs(b).max(1)
    byte = np.clip(np.where(amax > 0, np.frexp(amax)[1] - 1 + 127 - 7, 1), 1, 254)
    codes = (b * np.exp2(127.0 - byte)[:, None, :]).reshape(n, m).astype(np.float32).astype(ml_dtypes.float8_e4m3fn).view(np.uint8)
    words = codes.reshape(n // 512, 128, 4, m).transpose(0, 1, 3, 2)
    return np.ascontiguousarray(words), np.ascontiguousarray(byte.astype(np.uint8).reshape(n // 512, 16, m))


M, K, F, N = 1024, 1024, 2048, 1024


def setup_inputs():
    s = mx_kscale(K)
    t = mx_kscale(F)
    feats = np.random.randn(K, M)
    common = np.random.randn(K, 1)
    coef = (common + np.random.randn(K, F)) / np.sqrt(K)
    severity = np.exp(0.5 * np.random.randn(F))
    exposure = np.exp(2.0 * np.random.randn(F, N) - 1.0) / F
    capital = np.exp(0.8 * np.random.randn(N))
    x_words, x_scales = pack_weight(feats * s[:, None], "e4m3")
    coef_words, coef_scales = pack4(coef / s[:, None])
    return {"x_words": x_words, "x_scales": x_scales,
            "coef_words": coef_words, "coef_scales": coef_scales,
            "severity": bf(severity * t),
            "exposure": bf(exposure / t[:, None]),
            "capital": bf(capital)}

def reference(x_words, x_scales, coef_words, coef_scales, severity, exposure, capital):
    x = unpack_weight(x_words, x_scales, "e4m3")
    c = unpack4(coef_words, coef_scales)
    z = x.T @ c
    h = 1.0 / (1.0 + np.exp(-z)) * f64(severity)
    loss = mxq(h, 1, "e4m3") @ mxq(f64(exposure), 0, "e4m3")
    y = np.log(1.0 + loss) * f64(capital)
    words, scales = planes(y.T)
    return y, words, scales

@@ -1,0 +1,552 @@
+from contextlib import ExitStack
+
+import concourse.mybir as mybir
+from concourse.masks import make_identity
+
+M, K, F, N = 1024, 1024, 2048, 1024
+FLOPS = 2 * M * K * F + 2 * M * F * N
+
+F32 = mybir.dt.float32
+BF16 = mybir.dt.bfloat16
+I32 = mybir.dt.int32
+U32 = mybir.dt.uint32
+U8 = mybir.dt.uint8
+FP8X4 = mybir.dt.float8_e4m3fn_x4
+FP4X4 = mybir.dt.float4_e2m1fn_x4
+ACT = mybir.ActivationFunctionType
+MULT = mybir.AluOpType.mult
+ADD = mybir.AluOpType.add
+
+P = 128
+W = 512
+KG = K // W
+FG = F // W
+SIG_RING = 5
+E_ENG = 'VVVSVSVSVSSSVSSS'
+R_ENG = 'VVVVVVVVVSSSSSVV'
+GROUPS = [[0, 1], [2, 3], [4, 5], [6, 7], [8, 9], [10, 11], [12, 13], [14], [15]]
+ACC = [4, 5, 6, 7, 2, 3, 4, 5, 6, 7, 2, 3, 4, 5, 6, 7]
+TURN = [1, 1, 1, 1, 1, 0, 1, 0, 1]
+E_SLOT = [0, 1, 2, 3, 0, 4, 2, 1, 4, 3, 0, 3, 2, 1, 4, 0]
+ORDER = [
+    ('head',),
+    ('oc', 0),
+    ('os', 0, 2),
+    ('ov',),
+    ('e', 0, 1),
+    ('oc', 1),
+    ('z', 0, 2),
+    ('z', 0, 0),
+    ('z', 0, 1),
+    ('sg', 0, 2),
+    ('sg', 0, 0),
+    ('sg', 0, 1),
+    ('z', 0, 3),
+    ('tv',),
+    ('z', 1, 0),
+    ('z', 1, 1),
+    ('e', 0, 3),
+    ('sg', 0, 3),
+    ('sg', 1, 0),
+    ('e', 0, 2),
+    ('oc', 2),
+    ('os', 2, 4),
+    ('qe', 0, 1),
+    ('qe', 0, 2),
+    ('qe', 0, 3),
+    ('w', 0),
+    ('e', 0, 0),
+    ('oc', 3),
+    ('qe', 0, 0),
+    ('z', 1, 2),
+    ('z', 1, 3),
+    ('sg', 1, 1),
+    ('sg', 1, 2),
+    ('z', 2, 0),
+    ('sg', 1, 3),
+    ('z', 2, 1),
+    ('z', 2, 2),
+    ('sg', 2, 0),
+    ('sg', 2, 1),
+    ('sg', 2, 2),
+    ('qh', 0),
+    ('e', 1, 0),
+    ('e', 1, 2),
+    ('z', 2, 3),
+    ('z', 3, 1),
+    ('z', 3, 0),
+    ('e', 1, 3),
+    ('sg', 3, 1),
+    ('sg', 2, 3),
+    ('e', 1, 1),
+    ('sg', 3, 0),
+    ('l', 3, 0),
+    ('l', 0, 0),
+    ('z', 4, 0),
+    ('z', 3, 2),
+    ('z', 3, 3),
+    ('sg', 4, 0),
+    ('sg', 3, 2),
+    ('sg', 3, 3),
+    ('qe', 1, 3),
+    ('qe', 1, 2),
+    ('qe', 1, 0),
+    ('w', 2),
+    ('qe', 1, 1),
+    ('w', 1),
+    ('qh', 2),
+    ('e', 3, 0),
+    ('qh', 1),
+    ('l', 2, 0),
+    ('z', 4, 2),
+    ('z', 4, 3),
+    ('l', 1, 0),
+    ('z', 4, 1),
+    ('e', 3, 1),
+    ('e', 2, 1),
+    ('sg', 4, 2),
+    ('sg', 4, 3),
+    ('sg', 4, 1),
+    ('z', 5, 1),
+    ('z', 5, 2),
+    ('z', 5, 0),
+    ('l', 3, 1),
+    ('sg', 5, 1),
+    ('sg', 5, 2),
+    ('sg', 5, 0),
+    ('e', 2, 2),
+    ('z', 6, 0),
+    ('z', 5, 3),
+    ('z', 6, 1),
+    ('qe', 2, 1),
+    ('w', 3),
+    ('e', 2, 0),
+    ('qe', 2, 0),
+    ('qe', 3, 0),
+    ('qe', 2, 2),
+    ('qe', 3, 1),
+    ('w', 4),
+    ('qh', 3),
+    ('sg', 6, 0),
+    ('sg', 6, 1),
+    ('e', 3, 2),
+    ('sg', 5, 3),
+    ('e', 2, 3),
+    ('l', 2, 1),
+    ('z', 7, 0),
+    ('l', 1, 1),
+    ('l', 1, 2),
+    ('z', 6, 3),
+    ('z', 6, 2),
+    ('l', 0, 1),
+    ('l', 3, 2),
+    ('sg', 6, 3),
+    ('sg', 7, 0),
+    ('sg', 6, 2),
+    ('e', 3, 3),
+    ('qh', 4),
+    ('w', 5),
+    ('qh', 5),
+    ('qe', 2, 3),
+    ('qe', 3, 2),
+    ('qe', 3, 3),
+    ('w', 6),
+    ('qh', 6),
+    ('z', 7, 2),
+    ('l', 2, 2),
+    ('z', 7, 3),
+    ('l', 2, 3),
+    ('z', 7, 1),
+    ('l', 0, 2),
+    ('l', 0, 3),
+    ('sg', 7, 2),
+    ('sg', 7, 3),
+    ('sg', 7, 1),
+    ('ln', 0),
+    ('l', 4, 0),
+    ('l', 1, 3),
+    ('l', 5, 0),
+    ('l', 5, 1),
+    ('l', 4, 1),
+    ('l', 5, 2),
+    ('l', 4, 2),
+    ('l', 5, 3),
+    ('l', 3, 3),
+    ('l', 4, 3),
+    ('l', 6, 0),
+    ('ln', 1),
+    ('ln', 3),
+    ('ln', 2),
+    ('ln', 5),
+    ('y', 0),
+    ('y', 3),
+    ('y', 1),
+    ('r', 0),
+    ('r', 3),
+    ('r', 1),
+    ('w', 7),
+    ('y', 2),
+    ('r', 2),
+    ('qh', 7),
+    ('y', 5),
+    ('sy', 1),
+    ('sy', 0),
+    ('sy', 2),
+    ('sy', 3),
+    ('l', 6, 1),
+    ('l', 7, 0),
+    ('l', 6, 2),
+    ('l', 9, 0),
+    ('l', 6, 3),
+    ('l', 7, 1),
+    ('l', 7, 2),
+    ('l', 8, 0),
+    ('ln', 6),
+    ('ln', 4),
+    ('l', 7, 3),
+    ('l', 8, 1),
+    ('l', 9, 1),
+    ('l', 11, 0),
+    ('l', 12, 0),
+    ('l', 8, 2),
+    ('t', 0),
+    ('l', 10, 0),
+    ('sp', 0),
+    ('ln', 7),
+    ('y', 6),
+    ('y', 4),
+    ('y', 7),
+    ('r', 5),
+    ('qy', 0),
+    ('r', 4),
+    ('sy', 6),
+    ('sy', 5),
+    ('sy', 7),
+    ('sy', 4),
+    ('l', 11, 1),
+    ('l', 9, 2),
+    ('l', 11, 2),
+    ('l', 12, 1),
+    ('l', 10, 1),
+    ('l', 12, 2),
+    ('l', 12, 3),
+    ('t', 1),
+    ('l', 10, 2),
+    ('l', 8, 3),
+    ('l', 13, 0),
+    ('l', 9, 3),
+    ('l', 10, 3),
+    ('l', 11, 3),
+    ('l', 13, 1),
+    ('l', 13, 2),
+    ('ln', 12),
+    ('sp', 1),
+    ('ln', 8),
+    ('ln', 9),
+    ('ln', 11),
+    ('l', 13, 3),
+    ('l', 14, 0),
+    ('t', 2),
+    ('l', 14, 1),
+    ('l', 14, 2),
+    ('l', 14, 3),
+    ('ln', 10),
+    ('ln', 13),
+    ('sp', 2),
+    ('r', 7),
+    ('y', 9),
+    ('r', 6),
+    ('qy', 1),
+    ('y', 8),
+    ('y', 11),
+    ('r', 8),
+    ('y', 10),
+    ('y', 12),
+    ('y', 13),
+    ('t', 3),
+    ('l', 15, 0),
+    ('l', 15, 1),
+    ('l', 15, 2),
+    ('r', 9),
+    ('ln', 14),
+    ('sp', 3),
+    ('r', 11),
+    ('r', 10),
+    ('sy', 9),
+    ('sy', 8),
+    ('sc', 0, 0, 512),
+    ('sy', 11),
+    ('sy', 13),
+    ('l', 15, 3),
+    ('t', 4),
+    ('t', 5),
+    ('sp', 4),
+    ('r', 12),
+    ('ln', 15),
+    ('r', 13),
+    ('y', 14),
+    ('qy', 3),
+    ('qy', 2),
+    ('r', 14),
+    ('y', 15),
+    ('t', 6),
+    ('sp', 5),
+    ('sp', 6),
+    ('r', 15),
+    ('qy', 5),
+    ('qy', 4),
+    ('sy', 10),
+    ('sc', 1, 0, 512),
+    ('ss', 0, 1, 'P'),
+    ('ss', 0, 0, 'P'),
+    ('sy', 14),
+    ('ss', 0, 3, 'P'),
+    ('ss', 0, 2, 'P'),
+    ('sy', 12),
+    ('sy', 15),
+    ('sc', 0, 512, 1024),
+    ('t', 7),
+    ('t', 8),
+    ('sp', 7),
+    ('sp', 8),
+    ('qy', 6),
+    ('qy', 7),
+    ('qy', 8),
+    ('sc', 1, 512, 896),
+    ('sc', 1, 896, 1024),
+    ('ss', 1, 0, 'P'),
+    ('ss', 1, 2, 'P'),
+    ('ss', 1, 1, 'S'),
+    ('ss', 1, 3, 'S'),
+]
+LOADS = [('cs', 0, 2), ('c', 0), ('x', 0), ('xs',), ('sev',), ('e', 0), ('c', 1), ('c', 2), ('cs', 2, 4), ('e', 1), ('c', 3), ('x', 1), ('e', 2), ('e', 3), ('cap',)]
+
+
+def tile_sector_log_loss_capital_h2_kernel(
+    tc, x_words, x_scales, coef_words, coef_scales, severity, exposure, capital, out_0, out_1, out_2
+):
+    nc = tc.nc
+    with ExitStack() as ctx:
+        sb = ctx.enter_context(tc.tile_pool(name="sb", bufs=1))
+        ps = ctx.enter_context(tc.psum_pool(name="ps", bufs=1))
+        ctx.enter_context(tc.manual_schedule())
+
+        def tile(name, shape, dtype):
+            return sb.tile(shape, dtype, name=name, align_bytes=64)
+
+        bank = [ps.tile([P, W], F32, name="bank%d" % b) for b in range(8)]
+        x_codes = [tile("x_codes%d" % a, [P, KG, W], U32) for a in range(2)]
+        x_plane = tile("x_plane", [P, KG, M], U8)
+        c_raw = [tile("c_raw%d" % g, [P, KG, 2 * W], U8) for g in range(FG)]
+        c_codes = [tile("c_codes%d" % g, [P, 4, KG, 2 * P], U8) for g in range(FG)]
+        cs_raw = tile("cs_raw", [P, KG, F], U8)
+        c_plane = tile("c_plane", [P, KG, 4, FG, P], U8)
+        sev_row = tile("sev_row", [FG, W], BF16)
+        sev_pad = tile("sev_pad", [P, 4, P], F32)
+        ident = tile("ident", [P, P], F32)
+        one = tile("one", [P, 1], F32)
+        warm = tile("warm", [P, 1], F32)
+        cap = tile("cap", [P, N], BF16)
+        e_raw = [tile("e_raw%d" % g, [P, 4, N], BF16) for g in range(FG)]
+        e_bf = [tile("e_bf%d" % r, [P, W // 2, 4], BF16) for r in range(8)]
+        e_codes = [tile("e_codes%d" % g, [P, N], U32) for g in range(FG)]
+        e_plane = [tile("e_plane%d" % g, [P, N], U8) for g in range(FG)]
+        sig = [tile("sig%d" % r, [P, 4, W], F32) for r in range(SIG_RING)]
+        h_bf = [tile("h_bf%d" % r, [P, W, 4], BF16) for r in range(2)]
+        h_codes = [tile("h_codes%d" % u, [P, W], U32) for u in range(8)]
+        h_plane = [tile("h_plane%d" % u, [P, W], U8) for u in range(8)]
+        y = [tile("y%d" % r, [P, W], F32) for r in range(6)]
+        y_bf = [tile("y_bf%d" % r, [P, 2, P, 2], BF16) for r in range(4)]
+        yt = [tile("yt%d" % r, [P, W, 4], BF16) for r in range(2)]
+        y_codes = [tile("y_codes%d" % h, [P, M], U32) for h in range(2)]
+        y_plane = tile("y_plane", [P, 2, M], U8)
+
+        def load_x(a):
+            src = x_words.rearrange("g p m t -> p g (m t)")[:, :, 4 * W * a : 4 * W * (a + 1)]
+            nc.sync.dma_start(out=x_codes[a][:].bitcast(I32), in_=src.bitcast(I32))
+
+        def load_c(g):
+            src = coef_words.rearrange("g p b -> p g b")[:, :, 2 * W * g : 2 * W * (g + 1)]
+            nc.sync.dma_start(out=c_raw[g][:].bitcast(I32), in_=src.bitcast(I32))
+
+        def load_scales(plane, scales, c0, c1):
+            for q in range(4):
+                src = scales.rearrange("g r n -> r g n")[4 * q : 4 * q + 4, :, c0:c1]
+                nc.sync.dma_start(out=plane[32 * q : 32 * q + 4, :, c0:c1].bitcast(I32), in_=src.bitcast(I32))
+
+        def load_e(g, h0=0, h1=2):
+            rows = exposure[W * g : W * (g + 1), :].rearrange("(q t r) n -> t q r n", t=4, r=8)
+            for t in range(4):
+                nc.sync.dma_start(out=e_raw[g][:, t, W * h0 : W * h1], in_=rows[t][:, :, W * h0 : W * h1])
+
+        def order_c(g):
+            nc.vector.tensor_copy(
+                out=c_codes[g][:].bitcast(I32).rearrange("p t k (q w) -> p t (k q) w", w=4),
+                in_=c_raw[g][:].bitcast(I32).rearrange("p k (q t w) -> p t (k q) w", t=4, w=4),
+            )
+
+        def order_cs(g0, g1):
+            for k in range(KG):
+                nc.vector.tensor_copy(
+                    out=c_plane[:, k, :, g0:g1, :].bitcast(I32).rearrange("p t g (q w) -> p t (g q) w", w=2),
+                    in_=cs_raw[:, k, W * g0 : W * g1].bitcast(I32).rearrange("p (gq t w) -> p t gq w", t=4, w=2),
+                )
+
+        def score(u, t):
+            a, g = divmod(u, FG)
+            for k in range(KG):
+                nc.tensor.matmul_mx(
+                    out=bank[1 + (4 * u + t) % 3][:],
+                    lhsT=c_codes[g][:, t, k, :].bitcast(FP4X4),
+                    lhsT_scale=c_plane[:, k, t, g, :],
+                    rhs=x_codes[a][:, k, :].bitcast(FP8X4),
+                    rhs_scale=x_plane[:, k, W * a : W * (a + 1)],
+                    start=(k == 0),
+                    stop=(k == KG - 1),
+                )
+
+        def sigmoid(u, t):
+            nc.scalar.activation(out=sig[u % SIG_RING][:, t, :], in_=bank[1 + (4 * u + t) % 3][:], func=ACT.Sigmoid)
+
+        def order_sev():
+            nc.vector.tensor_copy(
+                out=sev_pad[0:FG].rearrange("g t (q r) -> g t q r", r=8),
+                in_=sev_row[:].rearrange("g (q t r) -> g t q r", t=4, r=8),
+            )
+
+        def turn_sev():
+            for t in range(4):
+                nc.tensor.transpose(bank[0][:, P * t : P * (t + 1)], sev_pad[:, t, :], ident[:])
+
+        def weigh(u):
+            g = u % FG
+            sev = bank[0][:].rearrange("p (t j) -> p t j", t=4)[:, :, g : g + 1]
+            nc.vector.tensor_tensor(
+                out=h_bf[u % 2][:].rearrange("p (c i) t -> p c t i", i=2),
+                in0=sig[u % SIG_RING][:].rearrange("p t (c i) -> p c t i", i=2),
+                in1=sev.unsqueeze(1).broadcast_to([P, W // 2, 4, 2]),
+                op=MULT,
+            )
+
+        def quant_h(u):
+            nc.vector.quantize_mx(
+                out=h_codes[u][:].bitcast(FP8X4), scales=h_plane[u][:], in_=h_bf[u % 2][:].rearrange("p m t -> p (m t)")
+            )
+
+        def move(engine, dst, src):
+            if engine == "V":
+                nc.vector.tensor_copy(out=dst, in_=src)
+            elif engine == "S":
+                nc.scalar.copy(out=dst, in_=src)
+            else:
+                nc.gpsimd.tensor_scalar(out=dst, in0=src, scalar1=1.0, scalar2=0.0, op0=MULT, op1=ADD)
+
+        def weave_e(g, j):
+            dst = e_bf[E_SLOT[4 * g + j]][:].rearrange("p (c i) t -> p c t i", i=4)
+            src = e_raw[g][:, :, 256 * j : 256 * (j + 1)].rearrange("p t (c i) -> p c t i", i=4)
+            move(E_ENG[4 * g + j], dst, src)
+
+        def quant_e(g, j):
+            cols = slice(256 * j, 256 * (j + 1))
+            nc.vector.quantize_mx(
+                out=e_codes[g][:, cols].bitcast(FP8X4),
+                scales=e_plane[g][:, cols],
+                in_=e_bf[E_SLOT[4 * g + j]][:].rearrange("p n t -> p (n t)"),
+            )
+
+        units = [(4 * a + i, h) for a in range(2) for h in range(2) for i in range(4)]
+
+        def loss(v, g):
+            i, h = units[v]
+            u = FG * (i // 4) + g
+            rows = slice(P * (i % 4), P * (i % 4 + 1))
+            cols = slice(W * h, W * (h + 1))
+            nc.tensor.matmul_mx(
+                out=bank[ACC[v]][:],
+                lhsT=h_codes[u][:, rows].bitcast(FP8X4),
+                lhsT_scale=h_plane[u][:, rows],
+                rhs=e_codes[g][:, cols].bitcast(FP8X4),
+                rhs_scale=e_plane[g][:, cols],
+                start=(g == 0),
+                stop=(g == FG - 1),
+            )
+
+        def logs(v):
+            return sig[(3 + v // 4) % SIG_RING][:, v % 4, :]
+
+        def log1p(v):
+            nc.scalar.activation(out=logs(v), in_=bank[ACC[v]][:], func=ACT.Ln, bias=one[:])
+
+        def scale_y(v):
+            h = units[v][1]
+            nc.vector.tensor_tensor(out=y[v % 6][:], in0=logs(v), in1=cap[:, W * h : W * (h + 1)], op=MULT)
+
+        def store_y(v):
+            i, h = units[v]
+            nc.sync.dma_start(out=out_0[P * i : P * (i + 1), W * h : W * (h + 1)], in_=y[v % 6][:])
+
+        def round_y(v):
+            move(R_ENG[v], y_bf[v % 4][:], y[v % 6][:].rearrange("m (p u e) -> m u p e", u=2, e=2))
+
+        def turn(k):
+            for s, v in enumerate(GROUPS[k]):
+                words = y_bf[v % 4][:].rearrange("m u p e -> m u (p e)").bitcast(F32)
+                for u in range(2):
+                    c = P * (2 * s + u)
+                    nc.tensor.transpose(bank[TURN[k]][:, c : c + P], words[:, u, :], ident[:])
+
+        def turned(k):
+            v, n = GROUPS[k][0], len(GROUPS[k])
+            return yt[(v // 4) % 2][:, P * (v % 4) : P * (v % 4 + n), :].rearrange("p m t -> p (m t)")
+
+        def spill(k):
+            n = len(GROUPS[k])
+            nc.scalar.copy(
+                out=turned(k).bitcast(F32).rearrange("p (s m u) -> p s m u", s=n, u=2),
+                in_=bank[TURN[k]][:, : 2 * P * n].rearrange("p (s u m) -> p s m u", s=n, u=2),
+            )
+
+        def quant_y(k):
+            i, h = units[GROUPS[k][0]]
+            cols = slice(P * i, P * (i + len(GROUPS[k])))
+            nc.vector.quantize_mx(out=y_codes[h][:, cols].bitcast(FP8X4), scales=y_plane[:, h, cols], in_=turned(k))
+
+        def store_codes(h, m0, m1):
+            dst = out_1[h].rearrange("p m t -> p (m t)")[:, 4 * m0 : 4 * m1]
+            nc.sync.dma_start(out=dst.bitcast(I32), in_=y_codes[h][:, m0:m1].bitcast(I32))
+
+        def store_scales(a, q, engine):
+            dst = out_2.rearrange("g r m -> r g m")[4 * q : 4 * q + 4, :, W * a : W * (a + 1)]
+            src = y_plane[32 * q : 32 * q + 4, :, W * a : W * (a + 1)]
+            (nc.scalar if engine == "S" else nc.sync).dma_start(out=dst.bitcast(I32), in_=src.bitcast(I32))
+
+        def head():
+            nc.vector.memset(cs_raw[:, :, 0 : 2 * W].bitcast(I32), 0)
+            nc.vector.memset(x_plane[:].bitcast(I32), 0)
+            nc.vector.memset(one[:], 1.0)
+            nc.vector.memset(cs_raw[:, :, 2 * W : F].bitcast(I32), 0)
+            nc.vector.memset(sev_pad[:], 0.0)
+            make_identity(nc, ident[:])
+            nc.scalar.activation(out=warm[:], in_=one[:], func=ACT.Sigmoid)
+            for step in LOADS:
+                loads[step[0]](*step[1:])
+
+        def load_sev():
+            nc.sync.dma_start(out=sev_row[:], in_=severity.rearrange("(g f) -> g f", g=FG))
+
+        def load_cap():
+            nc.sync.dma_start(out=cap[:], in_=capital.partition_broadcast(P))
+
+        loads = {
+            "x": load_x, "c": load_c, "e": load_e, "sev": load_sev, "cap": load_cap,
+            "cs": lambda g0, g1: load_scales(cs_raw, coef_scales, W * g0, W * g1),
+            "xs": lambda: load_scales(x_plane, x_scales, 0, M),
+        }
+
+        calls = {
+            "head": head, "oc": order_c, "os": order_cs, "ov": order_sev, "tv": turn_sev, "z": score, "sg": sigmoid,
+            "w": weigh, "qh": quant_h, "e": weave_e, "qe": quant_e, "l": loss, "ln": log1p, "y": scale_y,
+            "sy": store_y, "r": round_y, "t": turn, "sp": spill, "qy": quant_y, "sc": store_codes, "ss": store_scales,
+        }
+        for step in ORDER:
+            calls[step[0]](*step[1:])

@@ -22,304 +22,271 @@ W = 512
 KG = K // W
 FG = F // W
 SIG_RING = 5
-E_ENG = 'VVVSVSVSVSSSVSSS'
-R_ENG = 'VVVVVVVVVSSSSSVV'
+Y_RING = 4
+C_RUNS = [(0, 1), (1, 2), (2, 4)]
+R_ENG = 'SVSVVVSVV'
 GROUPS = [[0, 1], [2, 3], [4, 5], [6, 7], [8, 9], [10, 11], [12, 13], [14], [15]]
 ACC = [4, 5, 6, 7, 2, 3, 4, 5, 6, 7, 2, 3, 4, 5, 6, 7]
 TURN = [1, 1, 1, 1, 1, 0, 1, 0, 1]
-E_SLOT = [0, 1, 2, 3, 0, 4, 2, 1, 4, 3, 0, 3, 2, 1, 4, 0]
+E_SLOT = [0, 2, 2, 3, 2, 0, 3, 2]
 ORDER = [
     ('head',),
-    ('oc', 0),
-    ('os', 0, 2),
-    ('ov',),
-    ('e', 0, 1),
-    ('oc', 1),
-    ('z', 0, 2),
-    ('z', 0, 0),
+    ('os', 0),
+    ('oc', 0, 1),
     ('z', 0, 1),
-    ('sg', 0, 2),
-    ('sg', 0, 0),
     ('sg', 0, 1),
-    ('z', 0, 3),
-    ('tv',),
-    ('z', 1, 0),
-    ('z', 1, 1),
-    ('e', 0, 3),
-    ('sg', 0, 3),
-    ('sg', 1, 0),
-    ('e', 0, 2),
-    ('oc', 2),
-    ('os', 2, 4),
-    ('qe', 0, 1),
-    ('qe', 0, 2),
-    ('qe', 0, 3),
-    ('w', 0),
-    ('e', 0, 0),
-    ('oc', 3),
+    ('oc', 1, 2),
+    ('e', 0, 1, 'G', 2, 4),
+    ('e', 0, 0, 'V', 0, 4),
+    ('z', 0, 0),
+    ('ov',),
     ('qe', 0, 0),
-    ('z', 1, 2),
-    ('z', 1, 3),
+    ('oc', 2, 4),
+    ('z', 0, 2),
+    ('os', 1),
+    ('z', 1, 0),
+    ('sg', 0, 0),
+    ('sg', 0, 2),
+    ('z', 0, 3),
+    ('sg', 1, 0),
+    ('sg', 0, 3),
+    ('z', 1, 1),
     ('sg', 1, 1),
-    ('sg', 1, 2),
-    ('z', 2, 0),
+    ('tv',),
+    ('z', 1, 3),
+    ('w', 0),
     ('sg', 1, 3),
-    ('z', 2, 1),
-    ('z', 2, 2),
+    ('z', 1, 2),
+    ('z', 2, 0),
+    ('sg', 1, 2),
     ('sg', 2, 0),
-    ('sg', 2, 1),
+    ('e', 0, 1, 'G', 0, 2),
+    ('z', 2, 2),
     ('sg', 2, 2),
-    ('qh', 0),
-    ('e', 1, 0),
-    ('e', 1, 2),
+    ('z', 2, 1),
     ('z', 2, 3),
+    ('sg', 2, 1),
     ('z', 3, 1),
-    ('z', 3, 0),
-    ('e', 1, 3),
-    ('sg', 3, 1),
-    ('sg', 2, 3),
-    ('e', 1, 1),
-    ('sg', 3, 0),
-    ('l', 3, 0),
-    ('l', 0, 0),
-    ('z', 4, 0),
-    ('z', 3, 2),
-    ('z', 3, 3),
-    ('sg', 4, 0),
-    ('sg', 3, 2),
-    ('sg', 3, 3),
-    ('qe', 1, 3),
-    ('qe', 1, 2),
-    ('qe', 1, 0),
-    ('w', 2),
-    ('qe', 1, 1),
     ('w', 1),
-    ('qh', 2),
-    ('e', 3, 0),
+    ('sg', 2, 3),
+    ('e', 1, 1, 'G', 0, 2),
+    ('qh', 0),
+    ('z', 3, 0),
+    ('sg', 3, 0),
     ('qh', 1),
+    ('z', 3, 3),
     ('l', 2, 0),
-    ('z', 4, 2),
+    ('sg', 3, 1),
+    ('z', 4, 0),
+    ('e', 1, 1, 'S', 2, 4),
+    ('sg', 4, 0),
+    ('qe', 0, 1),
+    ('z', 3, 2),
+    ('sg', 3, 3),
+    ('sg', 3, 2),
     ('z', 4, 3),
-    ('l', 1, 0),
+    ('l', 0, 0),
     ('z', 4, 1),
-    ('e', 3, 1),
-    ('e', 2, 1),
-    ('sg', 4, 2),
+    ('e', 2, 1, 'S', 0, 2),
     ('sg', 4, 3),
+    ('e', 1, 0, 'G', 0, 2),
+    ('e', 1, 0, 'G', 2, 4),
+    ('w', 2),
+    ('w', 3),
+    ('z', 4, 2),
     ('sg', 4, 1),
-    ('z', 5, 1),
-    ('z', 5, 2),
+    ('sg', 4, 2),
+    ('qh', 2),
+    ('e', 2, 1, 'S', 2, 4),
     ('z', 5, 0),
+    ('qh', 3),
+    ('z', 5, 2),
+    ('l', 3, 0),
+    ('qe', 1, 0),
+    ('sg', 5, 0),
+    ('z', 5, 1),
+    ('l', 1, 0),
+    ('z', 5, 3),
+    ('e', 2, 0, 'G', 0, 2),
     ('l', 3, 1),
     ('sg', 5, 1),
+    ('qe', 1, 1),
     ('sg', 5, 2),
-    ('sg', 5, 0),
-    ('e', 2, 2),
     ('z', 6, 0),
-    ('z', 5, 3),
+    ('sg', 5, 3),
     ('z', 6, 1),
-    ('qe', 2, 1),
-    ('w', 3),
-    ('e', 2, 0),
-    ('qe', 2, 0),
-    ('qe', 3, 0),
-    ('qe', 2, 2),
-    ('qe', 3, 1),
-    ('w', 4),
-    ('qh', 3),
+    ('e', 2, 0, 'G', 2, 4),
     ('sg', 6, 0),
     ('sg', 6, 1),
-    ('e', 3, 2),
-    ('sg', 5, 3),
-    ('e', 2, 3),
-    ('l', 2, 1),
-    ('z', 7, 0),
-    ('l', 1, 1),
-    ('l', 1, 2),
-    ('z', 6, 3),
     ('z', 6, 2),
-    ('l', 0, 1),
-    ('l', 3, 2),
-    ('sg', 6, 3),
-    ('sg', 7, 0),
-    ('sg', 6, 2),
-    ('e', 3, 3),
-    ('qh', 4),
+    ('e', 3, 0, 'S', 0, 2),
+    ('z', 7, 0),
+    ('z', 6, 3),
+    ('w', 4),
     ('w', 5),
-    ('qh', 5),
-    ('qe', 2, 3),
-    ('qe', 3, 2),
-    ('qe', 3, 3),
-    ('w', 6),
-    ('qh', 6),
-    ('z', 7, 2),
-    ('l', 2, 2),
+    ('l', 1, 1),
+    ('l', 0, 1),
+    ('sg', 7, 0),
+    ('qe', 2, 0),
+    ('e', 3, 0, 'G', 2, 4),
+    ('sg', 6, 2),
+    ('sg', 6, 3),
     ('z', 7, 3),
-    ('l', 2, 3),
+    ('qh', 5),
     ('z', 7, 1),
+    ('l', 3, 2),
     ('l', 0, 2),
-    ('l', 0, 3),
-    ('sg', 7, 2),
+    ('z', 7, 2),
     ('sg', 7, 3),
-    ('sg', 7, 1),
-    ('ln', 0),
-    ('l', 4, 0),
-    ('l', 1, 3),
-    ('l', 5, 0),
-    ('l', 5, 1),
-    ('l', 4, 1),
-    ('l', 5, 2),
-    ('l', 4, 2),
-    ('l', 5, 3),
+    ('qe', 3, 0),
+    ('e', 3, 1, 'V', 0, 2),
     ('l', 3, 3),
-    ('l', 4, 3),
-    ('l', 6, 0),
-    ('ln', 1),
+    ('l', 0, 3),
+    ('sg', 7, 1),
+    ('l', 2, 1),
+    ('qh', 4),
+    ('l', 2, 2),
+    ('l', 4, 0),
+    ('l', 5, 0),
+    ('qe', 2, 1),
+    ('l', 5, 1),
+    ('sg', 7, 2),
+    ('l', 1, 2),
+    ('l', 1, 3),
+    ('e', 3, 1, 'G', 2, 4),
     ('ln', 3),
+    ('w', 6),
+    ('l', 4, 1),
+    ('qe', 3, 1),
+    ('qh', 6),
+    ('ln', 0),
+    ('l', 2, 3),
     ('ln', 2),
-    ('ln', 5),
-    ('y', 0),
-    ('y', 3),
-    ('y', 1),
-    ('r', 0),
-    ('r', 3),
-    ('r', 1),
-    ('w', 7),
-    ('y', 2),
-    ('r', 2),
-    ('qh', 7),
-    ('y', 5),
-    ('sy', 1),
-    ('sy', 0),
-    ('sy', 2),
-    ('sy', 3),
-    ('l', 6, 1),
-    ('l', 7, 0),
-    ('l', 6, 2),
+    ('l', 4, 2),
     ('l', 9, 0),
+    ('l', 5, 2),
+    ('ln', 1),
+    ('l', 6, 0),
+    ('l', 6, 1),
+    ('l', 6, 2),
+    ('l', 4, 3),
+    ('w', 7),
+    ('l', 5, 3),
     ('l', 6, 3),
-    ('l', 7, 1),
-    ('l', 7, 2),
     ('l', 8, 0),
     ('ln', 6),
+    ('y', 0),
+    ('l', 7, 0),
+    ('l', 7, 1),
+    ('ln', 5),
     ('ln', 4),
-    ('l', 7, 3),
-    ('l', 8, 1),
-    ('l', 9, 1),
-    ('l', 11, 0),
+    ('l', 7, 2),
     ('l', 12, 0),
-    ('l', 8, 2),
-    ('t', 0),
-    ('l', 10, 0),
-    ('sp', 0),
-    ('ln', 7),
-    ('y', 6),
-    ('y', 4),
-    ('y', 7),
-    ('r', 5),
-    ('qy', 0),
-    ('r', 4),
-    ('sy', 6),
-    ('sy', 5),
-    ('sy', 7),
-    ('sy', 4),
-    ('l', 11, 1),
+    ('l', 7, 3),
+    ('l', 9, 1),
     ('l', 9, 2),
-    ('l', 11, 2),
-    ('l', 12, 1),
+    ('qh', 7),
+    ('sy', 0),
+    ('l', 8, 1),
+    ('l', 8, 2),
+    ('l', 11, 0),
+    ('ln', 7),
+    ('y', 1),
+    ('l', 10, 0),
     ('l', 10, 1),
-    ('l', 12, 2),
-    ('l', 12, 3),
-    ('t', 1),
-    ('l', 10, 2),
-    ('l', 8, 3),
-    ('l', 13, 0),
     ('l', 9, 3),
-    ('l', 10, 3),
-    ('l', 11, 3),
-    ('l', 13, 1),
-    ('l', 13, 2),
-    ('ln', 12),
-    ('sp', 1),
-    ('ln', 8),
+    ('r', 0),
+    ('l', 8, 3),
+    ('l', 12, 1),
     ('ln', 9),
-    ('ln', 11),
+    ('t', 0),
+    ('ln', 8),
+    ('y', 2),
+    ('r', 1),
+    ('sp', 0),
+    ('l', 13, 0),
+    ('y', 3),
+    ('l', 10, 2),
+    ('l', 10, 3),
+    ('l', 13, 1),
+    ('l', 15, 0),
+    ('sy', 1),
+    ('r', 2),
+    ('y', 4),
+    ('t', 1),
+    ('l', 13, 2),
+    ('l', 11, 1),
+    ('l', 11, 2),
     ('l', 13, 3),
-    ('l', 14, 0),
+    ('sp', 1),
+    ('r', 3),
+    ('ln', 10),
     ('t', 2),
+    ('l', 12, 2),
+    ('sp', 2),
+    ('sy', 3),
+    ('r', 4),
+    ('l', 11, 3),
+    ('sy', 2),
+    ('qy', 0, 4),
+    ('ln', 11),
+    ('t', 3),
+    ('sp', 3),
+    ('y', 5),
+    ('sy', 4),
+    ('l', 15, 1),
+    ('sc', 0, 0, 512),
+    ('ln', 13),
+    ('l', 15, 2),
+    ('l', 12, 3),
+    ('sy', 5),
+    ('ln', 12),
+    ('l', 15, 3),
+    ('qy', 4, 4),
+    ('y', 6),
+    ('r', 5),
+    ('t', 4),
+    ('ss', 0, 0, 'P'),
+    ('sp', 4),
+    ('l', 14, 0),
     ('l', 14, 1),
+    ('ln', 15),
+    ('ss', 0, 2, 'P'),
+    ('sc', 1, 0, 512),
+    ('sy', 6),
+    ('ss', 0, 1, 'P'),
     ('l', 14, 2),
     ('l', 14, 3),
-    ('ln', 10),
-    ('ln', 13),
-    ('sp', 2),
-    ('r', 7),
-    ('y', 9),
-    ('r', 6),
-    ('qy', 1),
-    ('y', 8),
-    ('y', 11),
-    ('r', 8),
-    ('y', 10),
-    ('y', 12),
-    ('y', 13),
-    ('t', 3),
-    ('l', 15, 0),
-    ('l', 15, 1),
-    ('l', 15, 2),
-    ('r', 9),
     ('ln', 14),
-    ('sp', 3),
-    ('r', 11),
-    ('r', 10),
-    ('sy', 9),
-    ('sy', 8),
-    ('sc', 0, 0, 512),
-    ('sy', 11),
-    ('sy', 13),
-    ('l', 15, 3),
-    ('t', 4),
+    ('y', 7),
+    ('sy', 7),
     ('t', 5),
-    ('sp', 4),
-    ('r', 12),
-    ('ln', 15),
-    ('r', 13),
-    ('y', 14),
-    ('qy', 3),
-    ('qy', 2),
-    ('r', 14),
-    ('y', 15),
-    ('t', 6),
+    ('r', 6),
+    ('y', 8),
     ('sp', 5),
-    ('sp', 6),
-    ('r', 15),
-    ('qy', 5),
-    ('qy', 4),
-    ('sy', 10),
-    ('sc', 1, 0, 512),
-    ('ss', 0, 1, 'P'),
-    ('ss', 0, 0, 'P'),
-    ('sy', 14),
-    ('ss', 0, 3, 'P'),
-    ('ss', 0, 2, 'P'),
-    ('sy', 12),
-    ('sy', 15),
-    ('sc', 0, 512, 1024),
+    ('t', 6),
+    ('r', 7),
     ('t', 7),
-    ('t', 8),
+    ('sp', 6),
     ('sp', 7),
+    ('r', 8),
+    ('ss', 0, 3, 'P'),
+    ('t', 8),
+    ('qy', 8, 4),
+    ('sy', 8),
+    ('qy', 12, 2),
     ('sp', 8),
-    ('qy', 6),
-    ('qy', 7),
-    ('qy', 8),
+    ('qy', 14, 1),
+    ('qy', 15, 1),
+    ('sc', 0, 512, 1024),
+    ('ss', 1, 3, 'S'),
+    ('ss', 1, 1, 'S'),
     ('sc', 1, 512, 896),
-    ('sc', 1, 896, 1024),
     ('ss', 1, 0, 'P'),
     ('ss', 1, 2, 'P'),
-    ('ss', 1, 1, 'S'),
-    ('ss', 1, 3, 'S'),
+    ('sc', 1, 896, 1024),
 ]
-LOADS = [('cs', 0, 2), ('c', 0), ('x', 0), ('xs',), ('sev',), ('e', 0), ('c', 1), ('c', 2), ('cs', 2, 4), ('e', 1), ('c', 3), ('x', 1), ('e', 2), ('e', 3), ('cap',)]
+LOADS = [('cs', 0), ('xs', 0, 2), ('c', 0), ('x', 0), ('xs', 2, 4), ('c', 1), ('f', 0), ('sev',), ('c', 2), ('c', 3), ('cs', 1), ('f', 1), ('e', 1), ('x', 1), ('e', 2), ('e', 3), ('cap',)]
 
 
 def tile_sector_log_loss_capital_h2_kernel(
@@ -337,29 +304,30 @@ def tile_sector_log_loss_capital_h2_kernel(
         bank = [ps.tile([P, W], F32, name="bank%d" % b) for b in range(8)]
         x_codes = [tile("x_codes%d" % a, [P, KG, W], U32) for a in range(2)]
         x_plane = tile("x_plane", [P, KG, M], U8)
-        c_raw = [tile("c_raw%d" % g, [P, KG, 2 * W], U8) for g in range(FG)]
-        c_codes = [tile("c_codes%d" % g, [P, 4, KG, 2 * P], U8) for g in range(FG)]
-        cs_raw = tile("cs_raw", [P, KG, F], U8)
-        c_plane = tile("c_plane", [P, KG, 4, FG, P], U8)
+        c_raw = tile("c_raw", [P, FG, KG, 2 * W], U8)
+        c_codes = {g0: tile("c_codes%d" % g0, [P, 4, g1 - g0, KG, 2 * P], U8) for g0, g1 in C_RUNS}
+        cs_raw = [tile("cs_raw%d" % b, [P, KG, 2 * W], U8) for b in range(2)]
+        c_plane = [tile("c_plane%d" % b, [P, KG, 4, 2, P], U8) for b in range(2)]
         sev_row = tile("sev_row", [FG, W], BF16)
         sev_pad = tile("sev_pad", [P, 4, P], F32)
         ident = tile("ident", [P, P], F32)
         one = tile("one", [P, 1], F32)
         warm = tile("warm", [P, 1], F32)
         cap = tile("cap", [P, N], BF16)
-        e_raw = [tile("e_raw%d" % g, [P, 4, N], BF16) for g in range(FG)]
-        e_bf = [tile("e_bf%d" % r, [P, W // 2, 4], BF16) for r in range(8)]
+        e_first = [tile("e_first%d" % h, [P, 4, W], BF16) for h in range(2)]
+        e_raw = {g: tile("e_raw%d" % g, [P, 4, N], BF16) for g in range(1, FG)}
+        e_bf = [tile("e_bf%d" % r, [P, W, 4], BF16) for r in range(max(E_SLOT) + 1)]
         e_codes = [tile("e_codes%d" % g, [P, N], U32) for g in range(FG)]
         e_plane = [tile("e_plane%d" % g, [P, N], U8) for g in range(FG)]
         sig = [tile("sig%d" % r, [P, 4, W], F32) for r in range(SIG_RING)]
         h_bf = [tile("h_bf%d" % r, [P, W, 4], BF16) for r in range(2)]
         h_codes = [tile("h_codes%d" % u, [P, W], U32) for u in range(8)]
         h_plane = [tile("h_plane%d" % u, [P, W], U8) for u in range(8)]
-        y = [tile("y%d" % r, [P, W], F32) for r in range(6)]
-        y_bf = [tile("y_bf%d" % r, [P, 2, P, 2], BF16) for r in range(4)]
+        y = [tile("y%d" % r, [P, 2, W], F32) for r in range(Y_RING)]
+        y_bf = [tile("y_bf%d" % r, [P, 2, 2 * P, 2], BF16) for r in range(3)]
         yt = [tile("yt%d" % r, [P, W, 4], BF16) for r in range(2)]
         y_codes = [tile("y_codes%d" % h, [P, M], U32) for h in range(2)]
-        y_plane = tile("y_plane", [P, 2, M], U8)
+        y_plane = [tile("y_plane%d" % a, [P, 2, W], U8) for a in range(2)]
 
         def load_x(a):
             src = x_words.rearrange("g p m t -> p g (m t)")[:, :, 4 * W * a : 4 * W * (a + 1)]
@@ -367,38 +335,45 @@ def tile_sector_log_loss_capital_h2_kernel(
 
         def load_c(g):
             src = coef_words.rearrange("g p b -> p g b")[:, :, 2 * W * g : 2 * W * (g + 1)]
-            nc.sync.dma_start(out=c_raw[g][:].bitcast(I32), in_=src.bitcast(I32))
+            nc.sync.dma_start(out=c_raw[:, g].bitcast(I32), in_=src.bitcast(I32))
 
-        def load_scales(plane, scales, c0, c1):
-            for q in range(4):
+        def load_scales(plane, scales, c0, c1, q0, q1):
+            for q in range(q0, q1):
                 src = scales.rearrange("g r n -> r g n")[4 * q : 4 * q + 4, :, c0:c1]
-                nc.sync.dma_start(out=plane[32 * q : 32 * q + 4, :, c0:c1].bitcast(I32), in_=src.bitcast(I32))
+                nc.sync.dma_start(out=plane[32 * q : 32 * q + 4].bitcast(I32), in_=src.bitcast(I32))
 
-        def load_e(g, h0=0, h1=2):
-            rows = exposure[W * g : W * (g + 1), :].rearrange("(q t r) n -> t q r n", t=4, r=8)
+        def e_rows(g):
+            return exposure[W * g : W * (g + 1), :].rearrange("(q t r) n -> t q r n", t=4, r=8)
+
+        def load_first(h):
             for t in range(4):
-                nc.sync.dma_start(out=e_raw[g][:, t, W * h0 : W * h1], in_=rows[t][:, :, W * h0 : W * h1])
+                nc.sync.dma_start(out=e_first[h][:, t, :], in_=e_rows(0)[t][:, :, W * h : W * (h + 1)])
 
-        def order_c(g):
+        def load_e(g):
+            for t in range(4):
+                nc.sync.dma_start(out=e_raw[g][:, t, :], in_=e_rows(g)[t])
+
+        def order_c(g0, g1):
             nc.vector.tensor_copy(
-                out=c_codes[g][:].bitcast(I32).rearrange("p t k (q w) -> p t (k q) w", w=4),
-                in_=c_raw[g][:].bitcast(I32).rearrange("p k (q t w) -> p t (k q) w", t=4, w=4),
+                out=c_codes[g0][:].bitcast(I32).rearrange("p t g k (q w) -> p t (g k q) w", w=4),
+                in_=c_raw[:, g0:g1].bitcast(I32).rearrange("p g k (q t w) -> p t (g k q) w", t=4, w=4),
             )
 
-        def order_cs(g0, g1):
+        def order_cs(b):
             for k in range(KG):
                 nc.vector.tensor_copy(
-                    out=c_plane[:, k, :, g0:g1, :].bitcast(I32).rearrange("p t g (q w) -> p t (g q) w", w=2),
-                    in_=cs_raw[:, k, W * g0 : W * g1].bitcast(I32).rearrange("p (gq t w) -> p t gq w", t=4, w=2),
+                    out=c_plane[b][:, k].bitcast(I32).rearrange("p t g (q w) -> p t (g q) w", w=2),
+                    in_=cs_raw[b][:, k, :].bitcast(I32).rearrange("p (gq t w) -> p t gq w", t=4, w=2),
                 )
 
         def score(u, t):
             a, g = divmod(u, FG)
+            g0 = max(r[0] for r in C_RUNS if r[0] <= g)
             for k in range(KG):
                 nc.tensor.matmul_mx(
                     out=bank[1 + (4 * u + t) % 3][:],
-                    lhsT=c_codes[g][:, t, k, :].bitcast(FP4X4),
-                    lhsT_scale=c_plane[:, k, t, g, :],
+                    lhsT=c_codes[g0][:, t, g - g0, k, :].bitcast(FP4X4),
+                    lhsT_scale=c_plane[g // 2][:, k, t, g % 2, :],
                     rhs=x_codes[a][:, k, :].bitcast(FP8X4),
                     rhs_scale=x_plane[:, k, W * a : W * (a + 1)],
                     start=(k == 0),
@@ -441,17 +416,21 @@ def tile_sector_log_loss_capital_h2_kernel(
             else:
                 nc.gpsimd.tensor_scalar(out=dst, in0=src, scalar1=1.0, scalar2=0.0, op0=MULT, op1=ADD)
 
-        def weave_e(g, j):
-            dst = e_bf[E_SLOT[4 * g + j]][:].rearrange("p (c i) t -> p c t i", i=4)
-            src = e_raw[g][:, :, 256 * j : 256 * (j + 1)].rearrange("p t (c i) -> p c t i", i=4)
-            move(E_ENG[4 * g + j], dst, src)
+        def weave_e(g, h, engine, j0, j1):
+            dst = e_bf[E_SLOT[2 * g + h]][:, P * j0 : P * j1, :]
+            rows = e_first[h][:] if g == 0 else e_raw[g][:, :, W * h : W * (h + 1)]
+            src = rows[:, :, P * j0 : P * j1]
+            if engine == "G":
+                move(engine, dst, src.rearrange("p t c -> p c t"))
+            else:
+                move(engine, dst.rearrange("p (c i) t -> p c t i", i=4), src.rearrange("p t (c i) -> p c t i", i=4))
 
-        def quant_e(g, j):
-            cols = slice(256 * j, 256 * (j + 1))
+        def quant_e(g, h):
+            cols = slice(W * h, W * (h + 1))
             nc.vector.quantize_mx(
                 out=e_codes[g][:, cols].bitcast(FP8X4),
                 scales=e_plane[g][:, cols],
-                in_=e_bf[E_SLOT[4 * g + j]][:].rearrange("p n t -> p (n t)"),
+                in_=e_bf[E_SLOT[2 * g + h]][:].rearrange("p n t -> p (n t)"),
             )
 
         units = [(4 * a + i, h) for a in range(2) for h in range(2) for i in range(4)]
@@ -477,23 +456,33 @@ def tile_sector_log_loss_capital_h2_kernel(
         def log1p(v):
             nc.scalar.activation(out=logs(v), in_=bank[ACC[v]][:], func=ACT.Ln, bias=one[:])
 
-        def scale_y(v):
+        def scale_y(k):
+            v, n = GROUPS[k][0], len(GROUPS[k])
             h = units[v][1]
-            nc.vector.tensor_tensor(out=y[v % 6][:], in0=logs(v), in1=cap[:, W * h : W * (h + 1)], op=MULT)
+            nc.vector.tensor_tensor(
+                out=y[k % Y_RING][:, :n, :],
+                in0=sig[(3 + v // 4) % SIG_RING][:, v % 4 : v % 4 + n, :],
+                in1=cap[:, W * h : W * (h + 1)].unsqueeze(1).broadcast_to([P, n, W]),
+                op=MULT,
+            )
 
-        def store_y(v):
+        def store_y(k):
+            v, n = GROUPS[k][0], len(GROUPS[k])
             i, h = units[v]
-            nc.sync.dma_start(out=out_0[P * i : P * (i + 1), W * h : W * (h + 1)], in_=y[v % 6][:])
+            dst = out_0[P * i : P * (i + n), W * h : W * (h + 1)].rearrange("(s m) c -> m s c", s=n)
+            nc.sync.dma_start(out=dst, in_=y[k % Y_RING][:, :n, :])
 
-        def round_y(v):
-            move(R_ENG[v], y_bf[v % 4][:], y[v % 6][:].rearrange("m (p u e) -> m u p e", u=2, e=2))
+        def round_y(k):
+            n = len(GROUPS[k])
+            src = y[k % Y_RING][:, :n, :].rearrange("m s (p u e) -> m u (s p) e", u=2, e=2)
+            move(R_ENG[k], y_bf[k % 3][:, :, : P * n, :], src)
 
         def turn(k):
-            for s, v in enumerate(GROUPS[k]):
-                words = y_bf[v % 4][:].rearrange("m u p e -> m u (p e)").bitcast(F32)
+            words = y_bf[k % 3][:].rearrange("m u p e -> m u (p e)").bitcast(F32)
+            for s in range(len(GROUPS[k])):
                 for u in range(2):
                     c = P * (2 * s + u)
-                    nc.tensor.transpose(bank[TURN[k]][:, c : c + P], words[:, u, :], ident[:])
+                    nc.tensor.transpose(bank[TURN[k]][:, c : c + P], words[:, u, P * s : P * (s + 1)], ident[:])
 
         def turned(k):
             v, n = GROUPS[k][0], len(GROUPS[k])
@@ -506,10 +495,11 @@ def tile_sector_log_loss_capital_h2_kernel(
                 in_=bank[TURN[k]][:, : 2 * P * n].rearrange("p (s u m) -> p s m u", s=n, u=2),
             )
 
-        def quant_y(k):
-            i, h = units[GROUPS[k][0]]
-            cols = slice(P * i, P * (i + len(GROUPS[k])))
-            nc.vector.quantize_mx(out=y_codes[h][:, cols].bitcast(FP8X4), scales=y_plane[:, h, cols], in_=turned(k))
+        def quant_y(v, n):
+            i, h = units[v]
+            cols = slice(P * i, P * (i + n))
+            src = yt[(v // 4) % 2][:, P * (v % 4) : P * (v % 4 + n), :].rearrange("p m t -> p (m t)")
+            nc.vector.quantize_mx(out=y_codes[h][:, cols].bitcast(FP8X4), scales=y_plane[i // 4][:, h, P * (i % 4) : P * (i % 4 + n)], in_=src)
 
         def store_codes(h, m0, m1):
             dst = out_1[h].rearrange("p m t -> p (m t)")[:, 4 * m0 : 4 * m1]
@@ -517,14 +507,14 @@ def tile_sector_log_loss_capital_h2_kernel(
 
         def store_scales(a, q, engine):
             dst = out_2.rearrange("g r m -> r g m")[4 * q : 4 * q + 4, :, W * a : W * (a + 1)]
-            src = y_plane[32 * q : 32 * q + 4, :, W * a : W * (a + 1)]
+            src = y_plane[a][32 * q : 32 * q + 4]
             (nc.scalar if engine == "S" else nc.sync).dma_start(out=dst.bitcast(I32), in_=src.bitcast(I32))
 
         def head():
-            nc.vector.memset(cs_raw[:, :, 0 : 2 * W].bitcast(I32), 0)
+            nc.vector.memset(cs_raw[0][:].bitcast(I32), 0)
             nc.vector.memset(x_plane[:].bitcast(I32), 0)
             nc.vector.memset(one[:], 1.0)
-            nc.vector.memset(cs_raw[:, :, 2 * W : F].bitcast(I32), 0)
+            nc.vector.memset(cs_raw[1][:].bitcast(I32), 0)
             nc.vector.memset(sev_pad[:], 0.0)
             make_identity(nc, ident[:])
             nc.scalar.activation(out=warm[:], in_=one[:], func=ACT.Sigmoid)
@@ -539,8 +529,9 @@ def tile_sector_log_loss_capital_h2_kernel(
 
         loads = {
             "x": load_x, "c": load_c, "e": load_e, "sev": load_sev, "cap": load_cap,
-            "cs": lambda g0, g1: load_scales(cs_raw, coef_scales, W * g0, W * g1),
-            "xs": lambda: load_scales(x_plane, x_scales, 0, M),
+            "f": load_first,
+            "cs": lambda b: load_scales(cs_raw[b], coef_scales, 2 * W * b, 2 * W * (b + 1), 0, 4),
+            "xs": lambda q0, q1: load_scales(x_plane, x_scales, 0, M, q0, q1),
         }
 
         calls = {

@@ -21,272 +21,23 @@ P = 128
 W = 512
 KG = K // W
 FG = F // W
-SIG_RING = 5
-Y_RING = 4
+
+SIG_SLOTS = 5
+Y_SLOTS = 5
+ROUND_SLOTS = 3
+
 C_RUNS = [(0, 1), (1, 2), (2, 4)]
-R_ENG = 'SVSVVVSVV'
-GROUPS = [[0, 1], [2, 3], [4, 5], [6, 7], [8, 9], [10, 11], [12, 13], [14], [15]]
-ACC = [4, 5, 6, 7, 2, 3, 4, 5, 6, 7, 2, 3, 4, 5, 6, 7]
-TURN = [1, 1, 1, 1, 1, 0, 1, 0, 1]
-E_SLOT = [0, 2, 2, 3, 2, 0, 3, 2]
-ORDER = [
-    ('head',),
-    ('os', 0),
-    ('oc', 0, 1),
-    ('z', 0, 1),
-    ('sg', 0, 1),
-    ('oc', 1, 2),
-    ('e', 0, 1, 'G', 2, 4),
-    ('e', 0, 0, 'V', 0, 4),
-    ('z', 0, 0),
-    ('ov',),
-    ('qe', 0, 0),
-    ('oc', 2, 4),
-    ('z', 0, 2),
-    ('os', 1),
-    ('z', 1, 0),
-    ('sg', 0, 0),
-    ('sg', 0, 2),
-    ('z', 0, 3),
-    ('sg', 1, 0),
-    ('sg', 0, 3),
-    ('z', 1, 1),
-    ('sg', 1, 1),
-    ('tv',),
-    ('z', 1, 3),
-    ('w', 0),
-    ('sg', 1, 3),
-    ('z', 1, 2),
-    ('z', 2, 0),
-    ('sg', 1, 2),
-    ('sg', 2, 0),
-    ('e', 0, 1, 'G', 0, 2),
-    ('z', 2, 2),
-    ('sg', 2, 2),
-    ('z', 2, 1),
-    ('z', 2, 3),
-    ('sg', 2, 1),
-    ('z', 3, 1),
-    ('w', 1),
-    ('sg', 2, 3),
-    ('e', 1, 1, 'G', 0, 2),
-    ('qh', 0),
-    ('z', 3, 0),
-    ('sg', 3, 0),
-    ('qh', 1),
-    ('z', 3, 3),
-    ('l', 2, 0),
-    ('sg', 3, 1),
-    ('z', 4, 0),
-    ('e', 1, 1, 'S', 2, 4),
-    ('sg', 4, 0),
-    ('qe', 0, 1),
-    ('z', 3, 2),
-    ('sg', 3, 3),
-    ('sg', 3, 2),
-    ('z', 4, 3),
-    ('l', 0, 0),
-    ('z', 4, 1),
-    ('e', 2, 1, 'S', 0, 2),
-    ('sg', 4, 3),
-    ('e', 1, 0, 'G', 0, 2),
-    ('e', 1, 0, 'G', 2, 4),
-    ('w', 2),
-    ('w', 3),
-    ('z', 4, 2),
-    ('sg', 4, 1),
-    ('sg', 4, 2),
-    ('qh', 2),
-    ('e', 2, 1, 'S', 2, 4),
-    ('z', 5, 0),
-    ('qh', 3),
-    ('z', 5, 2),
-    ('l', 3, 0),
-    ('qe', 1, 0),
-    ('sg', 5, 0),
-    ('z', 5, 1),
-    ('l', 1, 0),
-    ('z', 5, 3),
-    ('e', 2, 0, 'G', 0, 2),
-    ('l', 3, 1),
-    ('sg', 5, 1),
-    ('qe', 1, 1),
-    ('sg', 5, 2),
-    ('z', 6, 0),
-    ('sg', 5, 3),
-    ('z', 6, 1),
-    ('e', 2, 0, 'G', 2, 4),
-    ('sg', 6, 0),
-    ('sg', 6, 1),
-    ('z', 6, 2),
-    ('e', 3, 0, 'S', 0, 2),
-    ('z', 7, 0),
-    ('z', 6, 3),
-    ('w', 4),
-    ('w', 5),
-    ('l', 1, 1),
-    ('l', 0, 1),
-    ('sg', 7, 0),
-    ('qe', 2, 0),
-    ('e', 3, 0, 'G', 2, 4),
-    ('sg', 6, 2),
-    ('sg', 6, 3),
-    ('z', 7, 3),
-    ('qh', 5),
-    ('z', 7, 1),
-    ('l', 3, 2),
-    ('l', 0, 2),
-    ('z', 7, 2),
-    ('sg', 7, 3),
-    ('qe', 3, 0),
-    ('e', 3, 1, 'V', 0, 2),
-    ('l', 3, 3),
-    ('l', 0, 3),
-    ('sg', 7, 1),
-    ('l', 2, 1),
-    ('qh', 4),
-    ('l', 2, 2),
-    ('l', 4, 0),
-    ('l', 5, 0),
-    ('qe', 2, 1),
-    ('l', 5, 1),
-    ('sg', 7, 2),
-    ('l', 1, 2),
-    ('l', 1, 3),
-    ('e', 3, 1, 'G', 2, 4),
-    ('ln', 3),
-    ('w', 6),
-    ('l', 4, 1),
-    ('qe', 3, 1),
-    ('qh', 6),
-    ('ln', 0),
-    ('l', 2, 3),
-    ('ln', 2),
-    ('l', 4, 2),
-    ('l', 9, 0),
-    ('l', 5, 2),
-    ('ln', 1),
-    ('l', 6, 0),
-    ('l', 6, 1),
-    ('l', 6, 2),
-    ('l', 4, 3),
-    ('w', 7),
-    ('l', 5, 3),
-    ('l', 6, 3),
-    ('l', 8, 0),
-    ('ln', 6),
-    ('y', 0),
-    ('l', 7, 0),
-    ('l', 7, 1),
-    ('ln', 5),
-    ('ln', 4),
-    ('l', 7, 2),
-    ('l', 12, 0),
-    ('l', 7, 3),
-    ('l', 9, 1),
-    ('l', 9, 2),
-    ('qh', 7),
-    ('sy', 0),
-    ('l', 8, 1),
-    ('l', 8, 2),
-    ('l', 11, 0),
-    ('ln', 7),
-    ('y', 1),
-    ('l', 10, 0),
-    ('l', 10, 1),
-    ('l', 9, 3),
-    ('r', 0),
-    ('l', 8, 3),
-    ('l', 12, 1),
-    ('ln', 9),
-    ('t', 0),
-    ('ln', 8),
-    ('y', 2),
-    ('r', 1),
-    ('sp', 0),
-    ('l', 13, 0),
-    ('y', 3),
-    ('l', 10, 2),
-    ('l', 10, 3),
-    ('l', 13, 1),
-    ('l', 15, 0),
-    ('sy', 1),
-    ('r', 2),
-    ('y', 4),
-    ('t', 1),
-    ('l', 13, 2),
-    ('l', 11, 1),
-    ('l', 11, 2),
-    ('l', 13, 3),
-    ('sp', 1),
-    ('r', 3),
-    ('ln', 10),
-    ('t', 2),
-    ('l', 12, 2),
-    ('sp', 2),
-    ('sy', 3),
-    ('r', 4),
-    ('l', 11, 3),
-    ('sy', 2),
-    ('qy', 0, 4),
-    ('ln', 11),
-    ('t', 3),
-    ('sp', 3),
-    ('y', 5),
-    ('sy', 4),
-    ('l', 15, 1),
-    ('sc', 0, 0, 512),
-    ('ln', 13),
-    ('l', 15, 2),
-    ('l', 12, 3),
-    ('sy', 5),
-    ('ln', 12),
-    ('l', 15, 3),
-    ('qy', 4, 4),
-    ('y', 6),
-    ('r', 5),
-    ('t', 4),
-    ('ss', 0, 0, 'P'),
-    ('sp', 4),
-    ('l', 14, 0),
-    ('l', 14, 1),
-    ('ln', 15),
-    ('ss', 0, 2, 'P'),
-    ('sc', 1, 0, 512),
-    ('sy', 6),
-    ('ss', 0, 1, 'P'),
-    ('l', 14, 2),
-    ('l', 14, 3),
-    ('ln', 14),
-    ('y', 7),
-    ('sy', 7),
-    ('t', 5),
-    ('r', 6),
-    ('y', 8),
-    ('sp', 5),
-    ('t', 6),
-    ('r', 7),
-    ('t', 7),
-    ('sp', 6),
-    ('sp', 7),
-    ('r', 8),
-    ('ss', 0, 3, 'P'),
-    ('t', 8),
-    ('qy', 8, 4),
-    ('sy', 8),
-    ('qy', 12, 2),
-    ('sp', 8),
-    ('qy', 14, 1),
-    ('qy', 15, 1),
-    ('sc', 0, 512, 1024),
-    ('ss', 1, 3, 'S'),
-    ('ss', 1, 1, 'S'),
-    ('sc', 1, 512, 896),
-    ('ss', 1, 0, 'P'),
-    ('ss', 1, 2, 'P'),
-    ('sc', 1, 896, 1024),
-]
-LOADS = [('cs', 0), ('xs', 0, 2), ('c', 0), ('x', 0), ('xs', 2, 4), ('c', 1), ('f', 0), ('sev',), ('c', 2), ('c', 3), ('cs', 1), ('f', 1), ('e', 1), ('x', 1), ('e', 2), ('e', 3), ('cap',)]
+
+E_CALLS = [[(0, 0)], [(0, 1)], [(1, 0), (1, 1)], [(3, 0), (2, 0)], [(2, 1)], [(3, 1)]]
+E_SLOT = {(0, 0): 0, (0, 1): 1, (1, 0): 1, (1, 1): 2, (3, 0): 1, (2, 0): 2, (2, 1): 0, (3, 1): 0}
+
+UNITS = [(4 * a + i, h) for a in range(2) for h in range(2) for i in range(4)]
+BATCHES = [(v, 2) for v in range(0, 14, 2)] + [(14, 1), (15, 1)]
+
+SEV_BANK = 0
+SCORE_BANKS = [1, 2, 3]
+LOSS_BANKS = [4, 5, 6, 7, 2, 3]
+TURN_BANKS = [1, 1, 1, 1, 1, 0, 1, 0, 1]
 
 
 def tile_sector_log_loss_capital_h2_kernel(
@@ -311,21 +62,22 @@ def tile_sector_log_loss_capital_h2_kernel(
         sev_row = tile("sev_row", [FG, W], BF16)
         sev_pad = tile("sev_pad", [P, 4, P], F32)
         ident = tile("ident", [P, P], F32)
+        large = tile("large", [P, 1], F32)
         one = tile("one", [P, 1], F32)
-        warm = tile("warm", [P, 1], F32)
         cap = tile("cap", [P, N], BF16)
         e_first = [tile("e_first%d" % h, [P, 4, W], BF16) for h in range(2)]
         e_raw = {g: tile("e_raw%d" % g, [P, 4, N], BF16) for g in range(1, FG)}
-        e_bf = [tile("e_bf%d" % r, [P, W, 4], BF16) for r in range(max(E_SLOT) + 1)]
-        e_codes = [tile("e_codes%d" % g, [P, N], U32) for g in range(FG)]
-        e_plane = [tile("e_plane%d" % g, [P, N], U8) for g in range(FG)]
-        sig = [tile("sig%d" % r, [P, 4, W], F32) for r in range(SIG_RING)]
-        h_bf = [tile("h_bf%d" % r, [P, W, 4], BF16) for r in range(2)]
-        h_codes = [tile("h_codes%d" % u, [P, W], U32) for u in range(8)]
-        h_plane = [tile("h_plane%d" % u, [P, W], U8) for u in range(8)]
-        y = [tile("y%d" % r, [P, 2, W], F32) for r in range(Y_RING)]
-        y_bf = [tile("y_bf%d" % r, [P, 2, 2 * P, 2], BF16) for r in range(3)]
-        yt = [tile("yt%d" % r, [P, W, 4], BF16) for r in range(2)]
+        e_bf = tile("e_bf", [P, 3, W, 4], BF16)
+        e_codes = [tile("e_codes%d" % c, [P, W * len(call)], U32) for c, call in enumerate(E_CALLS)]
+        e_plane = [tile("e_plane%d" % c, [P, W * len(call)], U8) for c, call in enumerate(E_CALLS)]
+        e_place = {block: (c, j) for c, call in enumerate(E_CALLS) for j, block in enumerate(call)}
+        sig = [tile("sig%d" % r, [P, 4, W], F32) for r in range(SIG_SLOTS)]
+        h_bf = tile("h_bf", [P, 2, W, 4], BF16)
+        h_codes = [tile("h_codes%d" % j, [P, 2 * W], U32) for j in range(4)]
+        h_plane = [tile("h_plane%d" % j, [P, 2 * W], U8) for j in range(4)]
+        y = [tile("y%d" % r, [P, 2, W], F32) for r in range(Y_SLOTS)]
+        y_bf = [tile("y_bf%d" % r, [P, 2, 2 * P, 2], BF16) for r in range(ROUND_SLOTS)]
+        y_turned = [tile("y_turned%d" % h, [P, W, 4], BF16) for h in range(2)]
         y_codes = [tile("y_codes%d" % h, [P, M], U32) for h in range(2)]
         y_plane = [tile("y_plane%d" % a, [P, 2, W], U8) for a in range(2)]
 
@@ -337,15 +89,15 @@ def tile_sector_log_loss_capital_h2_kernel(
             src = coef_words.rearrange("g p b -> p g b")[:, :, 2 * W * g : 2 * W * (g + 1)]
             nc.sync.dma_start(out=c_raw[:, g].bitcast(I32), in_=src.bitcast(I32))
 
-        def load_scales(plane, scales, c0, c1, q0, q1):
-            for q in range(q0, q1):
-                src = scales.rearrange("g r n -> r g n")[4 * q : 4 * q + 4, :, c0:c1]
+        def load_scales(plane, scales, cols, quadrants):
+            for q in quadrants:
+                src = scales.rearrange("g r n -> r g n")[4 * q : 4 * q + 4, :, cols]
                 nc.sync.dma_start(out=plane[32 * q : 32 * q + 4].bitcast(I32), in_=src.bitcast(I32))
 
         def e_rows(g):
             return exposure[W * g : W * (g + 1), :].rearrange("(q t r) n -> t q r n", t=4, r=8)
 
-        def load_first(h):
+        def load_e_first(h):
             for t in range(4):
                 nc.sync.dma_start(out=e_first[h][:, t, :], in_=e_rows(0)[t][:, :, W * h : W * (h + 1)])
 
@@ -353,191 +105,295 @@ def tile_sector_log_loss_capital_h2_kernel(
             for t in range(4):
                 nc.sync.dma_start(out=e_raw[g][:, t, :], in_=e_rows(g)[t])
 
-        def order_c(g0, g1):
+        def regroup_c(g0, g1):
             nc.vector.tensor_copy(
                 out=c_codes[g0][:].bitcast(I32).rearrange("p t g k (q w) -> p t (g k q) w", w=4),
                 in_=c_raw[:, g0:g1].bitcast(I32).rearrange("p g k (q t w) -> p t (g k q) w", t=4, w=4),
             )
 
-        def order_cs(b):
+        def regroup_c_scales(b):
             for k in range(KG):
                 nc.vector.tensor_copy(
                     out=c_plane[b][:, k].bitcast(I32).rearrange("p t g (q w) -> p t (g q) w", w=2),
                     in_=cs_raw[b][:, k, :].bitcast(I32).rearrange("p (gq t w) -> p t gq w", t=4, w=2),
                 )
 
-        def score(u, t):
-            a, g = divmod(u, FG)
-            g0 = max(r[0] for r in C_RUNS if r[0] <= g)
-            for k in range(KG):
-                nc.tensor.matmul_mx(
-                    out=bank[1 + (4 * u + t) % 3][:],
-                    lhsT=c_codes[g0][:, t, g - g0, k, :].bitcast(FP4X4),
-                    lhsT_scale=c_plane[g // 2][:, k, t, g % 2, :],
-                    rhs=x_codes[a][:, k, :].bitcast(FP8X4),
-                    rhs_scale=x_plane[:, k, W * a : W * (a + 1)],
-                    start=(k == 0),
-                    stop=(k == KG - 1),
-                )
-
-        def sigmoid(u, t):
-            nc.scalar.activation(out=sig[u % SIG_RING][:, t, :], in_=bank[1 + (4 * u + t) % 3][:], func=ACT.Sigmoid)
-
-        def order_sev():
+        def regroup_severity():
             nc.vector.tensor_copy(
                 out=sev_pad[0:FG].rearrange("g t (q r) -> g t q r", r=8),
                 in_=sev_row[:].rearrange("g (q t r) -> g t q r", t=4, r=8),
             )
 
-        def turn_sev():
+        def turn_severity():
             for t in range(4):
-                nc.tensor.transpose(bank[0][:, P * t : P * (t + 1)], sev_pad[:, t, :], ident[:])
+                nc.tensor.transpose(bank[SEV_BANK][:, P * t : P * (t + 1)], sev_pad[:, t, :], ident[:])
+
+        def score(u):
+            a, g = divmod(u, FG)
+            g0 = max(run[0] for run in C_RUNS if run[0] <= g)
+            for t in range(4):
+                z = bank[SCORE_BANKS[(4 * u + t) % len(SCORE_BANKS)]]
+                for k in range(KG):
+                    nc.tensor.matmul_mx(
+                        out=z[:],
+                        lhsT=c_codes[g0][:, t, g - g0, k, :].bitcast(FP4X4),
+                        lhsT_scale=c_plane[g // 2][:, k, t, g % 2, :],
+                        rhs=x_codes[a][:, k, :].bitcast(FP8X4),
+                        rhs_scale=x_plane[:, k, W * a : W * (a + 1)],
+                        start=(k == 0),
+                        stop=(k == KG - 1),
+                    )
+                nc.scalar.activation(out=sig[u % SIG_SLOTS][:, t, :], in_=z[:], func=ACT.Sigmoid)
 
         def weigh(u):
             g = u % FG
-            sev = bank[0][:].rearrange("p (t j) -> p t j", t=4)[:, :, g : g + 1]
+            sev = bank[SEV_BANK][:].rearrange("p (t j) -> p t j", t=4)[:, :, g : g + 1]
             nc.vector.tensor_tensor(
-                out=h_bf[u % 2][:].rearrange("p (c i) t -> p c t i", i=2),
-                in0=sig[u % SIG_RING][:].rearrange("p t (c i) -> p c t i", i=2),
+                out=h_bf[:, u % 2].rearrange("p (c i) t -> p c t i", i=2),
+                in0=sig[u % SIG_SLOTS][:].rearrange("p t (c i) -> p c t i", i=2),
                 in1=sev.unsqueeze(1).broadcast_to([P, W // 2, 4, 2]),
                 op=MULT,
             )
 
-        def quant_h(u):
-            nc.vector.quantize_mx(
-                out=h_codes[u][:].bitcast(FP8X4), scales=h_plane[u][:], in_=h_bf[u % 2][:].rearrange("p m t -> p (m t)")
-            )
+        def quant_h(j):
+            src = h_bf[:].rearrange("p s m t -> p (s m t)")
+            nc.vector.quantize_mx(out=h_codes[j][:].bitcast(FP8X4), scales=h_plane[j][:], in_=src)
 
-        def move(engine, dst, src):
-            if engine == "V":
-                nc.vector.tensor_copy(out=dst, in_=src)
-            elif engine == "S":
-                nc.scalar.copy(out=dst, in_=src)
-            else:
-                nc.gpsimd.tensor_scalar(out=dst, in0=src, scalar1=1.0, scalar2=0.0, op0=MULT, op1=ADD)
-
-        def weave_e(g, h, engine, j0, j1):
-            dst = e_bf[E_SLOT[2 * g + h]][:, P * j0 : P * j1, :]
+        def weave_views(g, h, c0, c1):
             rows = e_first[h][:] if g == 0 else e_raw[g][:, :, W * h : W * (h + 1)]
-            src = rows[:, :, P * j0 : P * j1]
-            if engine == "G":
-                move(engine, dst, src.rearrange("p t c -> p c t"))
-            else:
-                move(engine, dst.rearrange("p (c i) t -> p c t i", i=4), src.rearrange("p t (c i) -> p c t i", i=4))
+            return e_bf[:, E_SLOT[(g, h)], c0:c1, :], rows[:, :, c0:c1]
 
-        def quant_e(g, h):
-            cols = slice(W * h, W * (h + 1))
-            nc.vector.quantize_mx(
-                out=e_codes[g][:, cols].bitcast(FP8X4),
-                scales=e_plane[g][:, cols],
-                in_=e_bf[E_SLOT[2 * g + h]][:].rearrange("p n t -> p (n t)"),
+        def weave_by_fours(copy, g, h, c0, c1):
+            dst, src = weave_views(g, h, c0, c1)
+            copy(out=dst.rearrange("p (c i) t -> p c t i", i=4), in_=src.rearrange("p t (c i) -> p c t i", i=4))
+
+        def weave_gpsimd(g, h, c0, c1):
+            dst, src = weave_views(g, h, c0, c1)
+            nc.gpsimd.tensor_scalar(
+                out=dst, in0=src.rearrange("p t c -> p c t"), scalar1=1.0, scalar2=0.0, op0=MULT, op1=ADD
             )
 
-        units = [(4 * a + i, h) for a in range(2) for h in range(2) for i in range(4)]
+        def quant_e(c):
+            slot = E_SLOT[E_CALLS[c][0]]
+            src = e_bf[:, slot : slot + len(E_CALLS[c])].rearrange("p s n t -> p (s n t)")
+            nc.vector.quantize_mx(out=e_codes[c][:].bitcast(FP8X4), scales=e_plane[c][:], in_=src)
 
-        def loss(v, g):
-            i, h = units[v]
-            u = FG * (i // 4) + g
-            rows = slice(P * (i % 4), P * (i % 4 + 1))
+        def loss(units, groups):
+            for v in units:
+                i, h = UNITS[v]
+                for g in groups:
+                    u = FG * (i // 4) + g
+                    rows = slice(W * (u % 2) + P * (i % 4), W * (u % 2) + P * (i % 4 + 1))
+                    c, j = e_place[(g, h)]
+                    cols = slice(W * j, W * (j + 1))
+                    nc.tensor.matmul_mx(
+                        out=bank[LOSS_BANKS[v % len(LOSS_BANKS)]][:],
+                        lhsT=h_codes[u // 2][:, rows].bitcast(FP8X4),
+                        lhsT_scale=h_plane[u // 2][:, rows],
+                        rhs=e_codes[c][:, cols].bitcast(FP8X4),
+                        rhs_scale=e_plane[c][:, cols],
+                        start=(g == 0),
+                        stop=(g == FG - 1),
+                    )
+
+        def log_rows(v, n):
+            return sig[(3 + v // 4) % SIG_SLOTS][:, v % 4 : v % 4 + n, :]
+
+        def log1p(*units):
+            for v in units:
+                src = bank[LOSS_BANKS[v % len(LOSS_BANKS)]]
+                nc.scalar.activation(out=log_rows(v, 1)[:, 0, :], in_=src[:], func=ACT.Ln, bias=one[:])
+
+        def scale_and_store(k):
+            v, n = BATCHES[k]
+            i, h = UNITS[v]
             cols = slice(W * h, W * (h + 1))
-            nc.tensor.matmul_mx(
-                out=bank[ACC[v]][:],
-                lhsT=h_codes[u][:, rows].bitcast(FP8X4),
-                lhsT_scale=h_plane[u][:, rows],
-                rhs=e_codes[g][:, cols].bitcast(FP8X4),
-                rhs_scale=e_plane[g][:, cols],
-                start=(g == 0),
-                stop=(g == FG - 1),
-            )
-
-        def logs(v):
-            return sig[(3 + v // 4) % SIG_RING][:, v % 4, :]
-
-        def log1p(v):
-            nc.scalar.activation(out=logs(v), in_=bank[ACC[v]][:], func=ACT.Ln, bias=one[:])
-
-        def scale_y(k):
-            v, n = GROUPS[k][0], len(GROUPS[k])
-            h = units[v][1]
+            res = y[k % Y_SLOTS][:, :n, :]
             nc.vector.tensor_tensor(
-                out=y[k % Y_RING][:, :n, :],
-                in0=sig[(3 + v // 4) % SIG_RING][:, v % 4 : v % 4 + n, :],
-                in1=cap[:, W * h : W * (h + 1)].unsqueeze(1).broadcast_to([P, n, W]),
-                op=MULT,
+                out=res, in0=log_rows(v, n), in1=cap[:, cols].unsqueeze(1).broadcast_to([P, n, W]), op=MULT
             )
+            nc.sync.dma_start(out=out_0[P * i : P * (i + n), cols].rearrange("(s m) c -> m s c", s=n), in_=res)
 
-        def store_y(k):
-            v, n = GROUPS[k][0], len(GROUPS[k])
-            i, h = units[v]
-            dst = out_0[P * i : P * (i + n), W * h : W * (h + 1)].rearrange("(s m) c -> m s c", s=n)
-            nc.sync.dma_start(out=dst, in_=y[k % Y_RING][:, :n, :])
-
-        def round_y(k):
-            n = len(GROUPS[k])
-            src = y[k % Y_RING][:, :n, :].rearrange("m s (p u e) -> m u (s p) e", u=2, e=2)
-            move(R_ENG[k], y_bf[k % 3][:, :, : P * n, :], src)
+        def round_y(copy, k):
+            n = BATCHES[k][1]
+            src = y[k % Y_SLOTS][:, :n, :].rearrange("m s (p u e) -> m u (s p) e", u=2, e=2)
+            copy(out=y_bf[k % ROUND_SLOTS][:, :, : P * n, :], in_=src)
 
         def turn(k):
-            words = y_bf[k % 3][:].rearrange("m u p e -> m u (p e)").bitcast(F32)
-            for s in range(len(GROUPS[k])):
+            pairs = y_bf[k % ROUND_SLOTS][:].rearrange("m u p e -> m u (p e)").bitcast(F32)
+            for s in range(BATCHES[k][1]):
                 for u in range(2):
                     c = P * (2 * s + u)
-                    nc.tensor.transpose(bank[TURN[k]][:, c : c + P], words[:, u, P * s : P * (s + 1)], ident[:])
+                    nc.tensor.transpose(bank[TURN_BANKS[k]][:, c : c + P], pairs[:, u, P * s : P * (s + 1)], ident[:])
 
-        def turned(k):
-            v, n = GROUPS[k][0], len(GROUPS[k])
-            return yt[(v // 4) % 2][:, P * (v % 4) : P * (v % 4 + n), :].rearrange("p m t -> p (m t)")
+        def turned_rows(v, n):
+            return y_turned[UNITS[v][1]][:, P * (v % 4) : P * (v % 4 + n), :].rearrange("p m t -> p (m t)")
 
         def spill(k):
-            n = len(GROUPS[k])
+            v, n = BATCHES[k]
             nc.scalar.copy(
-                out=turned(k).bitcast(F32).rearrange("p (s m u) -> p s m u", s=n, u=2),
-                in_=bank[TURN[k]][:, : 2 * P * n].rearrange("p (s u m) -> p s m u", s=n, u=2),
+                out=turned_rows(v, n).bitcast(F32).rearrange("p (s m u) -> p s m u", s=n, u=2),
+                in_=bank[TURN_BANKS[k]][:, : 2 * P * n].rearrange("p (s u m) -> p s m u", s=n, u=2),
             )
 
         def quant_y(v, n):
-            i, h = units[v]
-            cols = slice(P * i, P * (i + n))
-            src = yt[(v // 4) % 2][:, P * (v % 4) : P * (v % 4 + n), :].rearrange("p m t -> p (m t)")
-            nc.vector.quantize_mx(out=y_codes[h][:, cols].bitcast(FP8X4), scales=y_plane[i // 4][:, h, P * (i % 4) : P * (i % 4 + n)], in_=src)
+            i, h = UNITS[v]
+            nc.vector.quantize_mx(
+                out=y_codes[h][:, P * i : P * (i + n)].bitcast(FP8X4),
+                scales=y_plane[i // 4][:, h, P * (i % 4) : P * (i % 4 + n)],
+                in_=turned_rows(v, n),
+            )
 
-        def store_codes(h, m0, m1):
-            dst = out_1[h].rearrange("p m t -> p (m t)")[:, 4 * m0 : 4 * m1]
-            nc.sync.dma_start(out=dst.bitcast(I32), in_=y_codes[h][:, m0:m1].bitcast(I32))
+        def store_codes(v, n):
+            i, h = UNITS[v]
+            dst = out_1[h].rearrange("p m t -> p (m t)")[:, 4 * P * i : 4 * P * (i + n)]
+            nc.sync.dma_start(out=dst.bitcast(I32), in_=y_codes[h][:, P * i : P * (i + n)].bitcast(I32))
 
-        def store_scales(a, q, engine):
-            dst = out_2.rearrange("g r m -> r g m")[4 * q : 4 * q + 4, :, W * a : W * (a + 1)]
-            src = y_plane[a][32 * q : 32 * q + 4]
-            (nc.scalar if engine == "S" else nc.sync).dma_start(out=dst.bitcast(I32), in_=src.bitcast(I32))
+        def store_scales(a, queues):
+            for q, queue in enumerate(queues):
+                dst = out_2.rearrange("g r m -> r g m")[4 * q : 4 * q + 4, :, W * a : W * (a + 1)]
+                queue.dma_start(out=dst.bitcast(I32), in_=y_plane[a][32 * q : 32 * q + 4].bitcast(I32))
 
-        def head():
-            nc.vector.memset(cs_raw[0][:].bitcast(I32), 0)
-            nc.vector.memset(x_plane[:].bitcast(I32), 0)
-            nc.vector.memset(one[:], 1.0)
-            nc.vector.memset(cs_raw[1][:].bitcast(I32), 0)
-            nc.vector.memset(sev_pad[:], 0.0)
-            make_identity(nc, ident[:])
-            nc.scalar.activation(out=warm[:], in_=one[:], func=ACT.Sigmoid)
-            for step in LOADS:
-                loads[step[0]](*step[1:])
+        on_vector, on_scalar = nc.vector.tensor_copy, nc.scalar.copy
+        half = W // 2
 
-        def load_sev():
-            nc.sync.dma_start(out=sev_row[:], in_=severity.rearrange("(g f) -> g f", g=FG))
+        nc.vector.memset(cs_raw[0][:].bitcast(I32), 0)
+        nc.vector.memset(x_plane[:].bitcast(I32), 0)
+        nc.vector.memset(large[:], 64.0)
+        nc.vector.memset(cs_raw[1][:].bitcast(I32), 0)
+        nc.vector.memset(sev_pad[:], 0.0)
+        nc.vector.memset(ident[:], 0.0)
+        make_identity(nc, ident[:], nomemset=True)
+        nc.scalar.activation(out=one[:], in_=large[:], func=ACT.Sigmoid)
+        nc.gpsimd.dma_start(out=sev_row[:], in_=severity.rearrange("(g f) -> g f", g=FG))
+        load_scales(cs_raw[0], coef_scales, slice(0, 2 * W), range(4))
+        load_scales(x_plane, x_scales, slice(0, M), range(2))
+        load_c(0)
+        load_x(0)
+        load_scales(x_plane, x_scales, slice(0, M), range(2, 4))
+        load_e_first(0)
+        for g in range(1, FG):
+            load_c(g)
+        load_scales(cs_raw[1], coef_scales, slice(2 * W, F), range(4))
+        load_e_first(1)
+        load_e(1)
+        load_x(1)
+        load_e(2)
+        load_e(3)
+        nc.sync.dma_start(out=cap[:], in_=capital.partition_broadcast(P))
 
-        def load_cap():
-            nc.sync.dma_start(out=cap[:], in_=capital.partition_broadcast(P))
+        regroup_c_scales(0)
+        regroup_c(*C_RUNS[0])
+        regroup_severity()
+        score(0)
+        turn_severity()
+        weave_by_fours(on_vector, 0, 0, 0, W)
+        regroup_c(*C_RUNS[1])
+        quant_e(0)
+        regroup_c(*C_RUNS[2])
+        regroup_c_scales(1)
+        for u in range(1, 4):
+            score(u)
 
-        loads = {
-            "x": load_x, "c": load_c, "e": load_e, "sev": load_sev, "cap": load_cap,
-            "f": load_first,
-            "cs": lambda b: load_scales(cs_raw[b], coef_scales, 2 * W * b, 2 * W * (b + 1), 0, 4),
-            "xs": lambda q0, q1: load_scales(x_plane, x_scales, 0, M, q0, q1),
-        }
+        weave_by_fours(on_scalar, 1, 1, half, W)
+        score(4)
+        weave_gpsimd(0, 1, 0, W)
+        weigh(0)
+        weigh(1)
+        quant_h(0)
+        quant_e(1)
 
-        calls = {
-            "head": head, "oc": order_c, "os": order_cs, "ov": order_sev, "tv": turn_sev, "z": score, "sg": sigmoid,
-            "w": weigh, "qh": quant_h, "e": weave_e, "qe": quant_e, "l": loss, "ln": log1p, "y": scale_y,
-            "sy": store_y, "r": round_y, "t": turn, "sp": spill, "qy": quant_y, "sc": store_codes, "ss": store_scales,
-        }
-        for step in ORDER:
-            calls[step[0]](*step[1:])
+        weave_by_fours(on_scalar, 2, 1, 0, half)
+        score(5)
+        loss(range(4), [0])
+        weave_gpsimd(1, 0, 0, W)
+        weave_gpsimd(1, 1, 0, half)
+        weigh(2)
+        weigh(3)
+        quant_h(1)
+        quant_e(2)
+
+        weave_by_fours(on_scalar, 2, 0, half, W)
+        score(6)
+        loss(range(4), [1])
+        weave_by_fours(on_scalar, 2, 1, half, W)
+        score(7)
+        weave_gpsimd(3, 0, 0, W)
+        weave_gpsimd(2, 0, 0, half)
+        weigh(4)
+        weigh(5)
+        quant_e(3)
+        quant_h(2)
+        quant_e(4)
+
+        loss(range(4), [2, 3])
+        loss([4, 5], [0, 1, 2])
+        log1p(0, 1, 2, 3)
+        loss([6, 7], [0, 1, 2])
+        loss([8, 9], [0, 1])
+        weave_gpsimd(3, 1, 0, W)
+        weigh(6)
+        weigh(7)
+        quant_e(5)
+
+        loss([4, 5, 6, 7], [3])
+        log1p(4, 5)
+        scale_and_store(0)
+        round_y(on_scalar, 0)
+        log1p(6, 7)
+        quant_h(3)
+        loss([10], [0, 1])
+        loss([8], [2, 3])
+        turn(0)
+        spill(0)
+        loss([9, 10], [2, 3])
+        log1p(8, 9, 10)
+        scale_and_store(1)
+        round_y(on_vector, 1)
+        turn(1)
+        spill(1)
+        scale_and_store(2)
+        round_y(on_scalar, 2)
+        loss([11, 12, 13], range(FG))
+        log1p(11, 12, 13)
+        turn(2)
+        spill(2)
+        scale_and_store(3)
+        scale_and_store(4)
+        round_y(on_vector, 3)
+        quant_y(0, 4)
+        scale_and_store(5)
+        round_y(on_scalar, 5)
+        loss([14], range(FG))
+        turn(3)
+        spill(3)
+        loss([15], range(FG))
+        log1p(14, 15)
+        scale_and_store(6)
+        round_y(on_vector, 4)
+        turn(4)
+        spill(4)
+        turn(5)
+        spill(5)
+        round_y(on_vector, 6)
+        quant_y(4, 4)
+        store_codes(0, 4)
+        store_codes(4, 4)
+        store_scales(0, [nc.sync] * 4)
+        scale_and_store(7)
+        scale_and_store(8)
+        turn(6)
+        spill(6)
+        round_y(on_vector, 7)
+        round_y(on_vector, 8)
+        for k in (7, 8):
+            turn(k)
+            spill(k)
+        quant_y(8, 4)
+        store_codes(8, 4)
+        quant_y(12, 2)
+        quant_y(14, 1)
+        store_codes(12, 3)
+        quant_y(15, 1)
+        store_codes(15, 1)
+        store_scales(1, [nc.sync, nc.scalar, nc.sync, nc.scalar])

@@ -37,7 +37,7 @@ BATCHES = [(v, 2) for v in range(0, 14, 2)] + [(14, 1), (15, 1)]
 SEV_BANK = 0
 SCORE_BANKS = [1, 2, 3]
 LOSS_BANKS = [4, 5, 6, 7, 2, 3]
-TURN_BANKS = [1, 1, 1, 1, 1, 0, 1, 0, 1]
+TURN_BANKS = [1, 1, 1, 1, 1, 0, 2, 3, 4]
 
 
 def tile_sector_log_loss_capital_h2_kernel(
@@ -111,11 +111,11 @@ def tile_sector_log_loss_capital_h2_kernel(
                 in_=c_raw[:, g0:g1].bitcast(I32).rearrange("p g k (q t w) -> p t (g k q) w", t=4, w=4),
             )
 
-        def regroup_c_scales(b):
+        def regroup_c_scales(b, parts):
             for k in range(KG):
                 nc.vector.tensor_copy(
-                    out=c_plane[b][:, k].bitcast(I32).rearrange("p t g (q w) -> p t (g q) w", w=2),
-                    in_=cs_raw[b][:, k, :].bitcast(I32).rearrange("p (gq t w) -> p t gq w", t=4, w=2),
+                    out=c_plane[b][parts, k].bitcast(I32).rearrange("p t g (q w) -> p t (g q) w", w=2),
+                    in_=cs_raw[b][parts, k, :].bitcast(I32).rearrange("p (gq t w) -> p t gq w", t=4, w=2),
                 )
 
         def regroup_severity():
@@ -257,12 +257,12 @@ def tile_sector_log_loss_capital_h2_kernel(
         on_vector, on_scalar = nc.vector.tensor_copy, nc.scalar.copy
         half = W // 2
 
-        nc.vector.memset(cs_raw[0][:].bitcast(I32), 0)
         nc.vector.memset(x_plane[:].bitcast(I32), 0)
         nc.vector.memset(large[:], 64.0)
+        nc.vector.memset(ident[:], 0.0)
+        nc.vector.memset(c_plane[0][:].bitcast(I32), 0)
         nc.vector.memset(cs_raw[1][:].bitcast(I32), 0)
         nc.vector.memset(sev_pad[:], 0.0)
-        nc.vector.memset(ident[:], 0.0)
         make_identity(nc, ident[:], nomemset=True)
         nc.scalar.activation(out=one[:], in_=large[:], func=ACT.Sigmoid)
         nc.gpsimd.dma_start(out=sev_row[:], in_=severity.rearrange("(g f) -> g f", g=FG))
@@ -282,7 +282,8 @@ def tile_sector_log_loss_capital_h2_kernel(
         load_e(3)
         nc.sync.dma_start(out=cap[:], in_=capital.partition_broadcast(P))
 
-        regroup_c_scales(0)
+        for q in range(4):
+            regroup_c_scales(0, slice(32 * q, 32 * q + 4))
         regroup_c(*C_RUNS[0])
         regroup_severity()
         score(0)
@@ -291,7 +292,7 @@ def tile_sector_log_loss_capital_h2_kernel(
         regroup_c(*C_RUNS[1])
         quant_e(0)
         regroup_c(*C_RUNS[2])
-        regroup_c_scales(1)
+        regroup_c_scales(1, slice(0, P))
         for u in range(1, 4):
             score(u)
 
@@ -392,8 +393,7 @@ def tile_sector_log_loss_capital_h2_kernel(
         quant_y(8, 4)
         store_codes(8, 4)
         quant_y(12, 2)
-        quant_y(14, 1)
-        store_codes(12, 3)
-        quant_y(15, 1)
-        store_codes(15, 1)
+        store_codes(12, 2)
+        quant_y(14, 2)
+        store_codes(14, 2)
         store_scales(1, [nc.sync, nc.scalar, nc.sync, nc.scalar])

@@ -79,7 +79,7 @@ def tile_sector_log_loss_capital_h2_kernel(
         y_bf = [tile("y_bf%d" % r, [P, 2, 2 * P, 2], BF16) for r in range(ROUND_SLOTS)]
         y_turned = [tile("y_turned%d" % h, [P, W, 4], BF16) for h in range(2)]
         y_codes = [tile("y_codes%d" % h, [P, M], U32) for h in range(2)]
-        y_plane = [tile("y_plane%d" % a, [P, 2, W], U8) for a in range(2)]
+        y_plane = tile("y_plane", [P, 2, M], U8)
 
         def load_x(a):
             src = x_words.rearrange("g p m t -> p g (m t)")[:, :, 4 * W * a : 4 * W * (a + 1)]
@@ -204,19 +204,22 @@ def tile_sector_log_loss_capital_h2_kernel(
                 src = bank[LOSS_BANKS[v % len(LOSS_BANKS)]]
                 nc.scalar.activation(out=log_rows(v, 1)[:, 0, :], in_=src[:], func=ACT.Ln, bias=one[:])
 
+        def y_rows(v, n):
+            return y[v // 2 % Y_SLOTS][:, v % 2 : v % 2 + n, :]
+
         def scale_and_store(k):
             v, n = BATCHES[k]
-            i, h = UNITS[v]
+            i, h = UNITS[v + n - 1]
             cols = slice(W * h, W * (h + 1))
-            res = y[k % Y_SLOTS][:, :n, :]
-            nc.vector.tensor_tensor(
-                out=res, in0=log_rows(v, n), in1=cap[:, cols].unsqueeze(1).broadcast_to([P, n, W]), op=MULT
-            )
-            nc.sync.dma_start(out=out_0[P * i : P * (i + n), cols].rearrange("(s m) c -> m s c", s=n), in_=res)
+            gain = cap[:, cols].unsqueeze(1).broadcast_to([P, n, W])
+            nc.vector.tensor_tensor(out=y_rows(v, n), in0=log_rows(v, n), in1=gain, op=MULT)
+            if i % 2 == 1:
+                dst = out_0[P * (i - 1) : P * (i + 1), cols].rearrange("(s m) c -> m s c", s=2)
+                nc.sync.dma_start(out=dst, in_=y_rows(v + n - 2, 2))
 
         def round_y(copy, k):
-            n = BATCHES[k][1]
-            src = y[k % Y_SLOTS][:, :n, :].rearrange("m s (p u e) -> m u (s p) e", u=2, e=2)
+            v, n = BATCHES[k]
+            src = y_rows(v, n).rearrange("m s (p u e) -> m u (s p) e", u=2, e=2)
             copy(out=y_bf[k % ROUND_SLOTS][:, :, : P * n, :], in_=src)
 
         def turn(k):
@@ -240,7 +243,7 @@ def tile_sector_log_loss_capital_h2_kernel(
             i, h = UNITS[v]
             nc.vector.quantize_mx(
                 out=y_codes[h][:, P * i : P * (i + n)].bitcast(FP8X4),
-                scales=y_plane[i // 4][:, h, P * (i % 4) : P * (i % 4 + n)],
+                scales=y_plane[:, h, P * i : P * (i + n)],
                 in_=turned_rows(v, n),
             )
 
@@ -249,10 +252,10 @@ def tile_sector_log_loss_capital_h2_kernel(
             dst = out_1[h].rearrange("p m t -> p (m t)")[:, 4 * P * i : 4 * P * (i + n)]
             nc.sync.dma_start(out=dst.bitcast(I32), in_=y_codes[h][:, P * i : P * (i + n)].bitcast(I32))
 
-        def store_scales(a, queues):
+        def store_scales(queues):
             for q, queue in enumerate(queues):
-                dst = out_2.rearrange("g r m -> r g m")[4 * q : 4 * q + 4, :, W * a : W * (a + 1)]
-                queue.dma_start(out=dst.bitcast(I32), in_=y_plane[a][32 * q : 32 * q + 4].bitcast(I32))
+                dst = out_2.rearrange("g r m -> r g m")[4 * q : 4 * q + 4]
+                queue.dma_start(out=dst.bitcast(I32), in_=y_plane[32 * q : 32 * q + 4].bitcast(I32))
 
         on_vector, on_scalar = nc.vector.tensor_copy, nc.scalar.copy
         half = W // 2
@@ -363,6 +366,7 @@ def tile_sector_log_loss_capital_h2_kernel(
         scale_and_store(4)
         round_y(on_vector, 3)
         quant_y(0, 4)
+        store_codes(0, 4)
         scale_and_store(5)
         round_y(on_scalar, 5)
         loss([14], range(FG))
@@ -378,9 +382,7 @@ def tile_sector_log_loss_capital_h2_kernel(
         spill(5)
         round_y(on_vector, 6)
         quant_y(4, 4)
-        store_codes(0, 4)
         store_codes(4, 4)
-        store_scales(0, [nc.sync] * 4)
         scale_and_store(7)
         scale_and_store(8)
         turn(6)
@@ -393,7 +395,8 @@ def tile_sector_log_loss_capital_h2_kernel(
         quant_y(8, 4)
         store_codes(8, 4)
         quant_y(12, 2)
-        store_codes(12, 2)
-        quant_y(14, 2)
-        store_codes(14, 2)
-        store_scales(1, [nc.sync, nc.scalar, nc.sync, nc.scalar])
+        quant_y(14, 1)
+        store_codes(12, 3)
+        quant_y(15, 1)
+        store_codes(15, 1)
+        store_scales([nc.sync, nc.scalar, nc.sync, nc.scalar])

from contextlib import ExitStack

import concourse.mybir as mybir
from concourse.masks import make_identity

M, K, F, N = 1024, 1024, 2048, 1024
FLOPS = 2 * M * K * F + 2 * M * F * N

F32 = mybir.dt.float32
BF16 = mybir.dt.bfloat16
I32 = mybir.dt.int32
U32 = mybir.dt.uint32
U8 = mybir.dt.uint8
FP8X4 = mybir.dt.float8_e4m3fn_x4
FP4X4 = mybir.dt.float4_e2m1fn_x4
ACT = mybir.ActivationFunctionType
MULT = mybir.AluOpType.mult
ADD = mybir.AluOpType.add

P = 128
W = 512
KG = K // W
FG = F // W

SIG_SLOTS = 5
Y_SLOTS = 5
ROUND_SLOTS = 3

C_RUNS = [(0, 1), (1, 2), (2, 4)]

E_CALLS = [[(0, 0)], [(0, 1)], [(1, 0), (1, 1)], [(3, 0), (2, 0)], [(2, 1)], [(3, 1)]]
E_SLOT = {(0, 0): 0, (0, 1): 1, (1, 0): 1, (1, 1): 2, (3, 0): 1, (2, 0): 2, (2, 1): 0, (3, 1): 0}

UNITS = [(4 * a + i, h) for a in range(2) for h in range(2) for i in range(4)]
BATCHES = [(v, 2) for v in range(0, 14, 2)] + [(14, 1), (15, 1)]

SEV_BANK = 0
SCORE_BANKS = [1, 2, 3]
LOSS_BANKS = [4, 5, 6, 7, 2, 3]
TURN_BANKS = [1, 1, 1, 1, 1, 0, 2, 3, 4]


def tile_sector_log_loss_capital_h2_kernel(
    tc, x_words, x_scales, coef_words, coef_scales, severity, exposure, capital, out_0, out_1, out_2
):
    nc = tc.nc
    with ExitStack() as ctx:
        sb = ctx.enter_context(tc.tile_pool(name="sb", bufs=1))
        ps = ctx.enter_context(tc.psum_pool(name="ps", bufs=1))
        ctx.enter_context(tc.manual_schedule())

        def tile(name, shape, dtype):
            return sb.tile(shape, dtype, name=name, align_bytes=64)

        bank = [ps.tile([P, W], F32, name="bank%d" % b) for b in range(8)]
        x_codes = [tile("x_codes%d" % a, [P, KG, W], U32) for a in range(2)]
        x_plane = tile("x_plane", [P, KG, M], U8)
        c_raw = tile("c_raw", [P, FG, KG, 2 * W], U8)
        c_codes = {g0: tile("c_codes%d" % g0, [P, 4, g1 - g0, KG, 2 * P], U8) for g0, g1 in C_RUNS}
        cs_raw = [tile("cs_raw%d" % b, [P, KG, 2 * W], U8) for b in range(2)]
        c_plane = [tile("c_plane%d" % b, [P, KG, 4, 2, P], U8) for b in range(2)]
        sev_row = tile("sev_row", [FG, W], BF16)
        sev_pad = tile("sev_pad", [P, 4, P], F32)
        ident = tile("ident", [P, P], F32)
        large = tile("large", [P, 1], F32)
        one = tile("one", [P, 1], F32)
        cap = tile("cap", [P, N], BF16)
        e_first = [tile("e_first%d" % h, [P, 4, W], BF16) for h in range(2)]
        e_raw = {g: tile("e_raw%d" % g, [P, 4, N], BF16) for g in range(1, FG)}
        e_bf = tile("e_bf", [P, 3, W, 4], BF16)
        e_codes = [tile("e_codes%d" % c, [P, W * len(call)], U32) for c, call in enumerate(E_CALLS)]
        e_plane = [tile("e_plane%d" % c, [P, W * len(call)], U8) for c, call in enumerate(E_CALLS)]
        e_place = {block: (c, j) for c, call in enumerate(E_CALLS) for j, block in enumerate(call)}
        sig = [tile("sig%d" % r, [P, 4, W], F32) for r in range(SIG_SLOTS)]
        h_bf = tile("h_bf", [P, 2, W, 4], BF16)
        h_codes = [tile("h_codes%d" % j, [P, 2 * W], U32) for j in range(4)]
        h_plane = [tile("h_plane%d" % j, [P, 2 * W], U8) for j in range(4)]
        y = [tile("y%d" % r, [P, 2, W], F32) for r in range(Y_SLOTS)]
        y_bf = [tile("y_bf%d" % r, [P, 2, 2 * P, 2], BF16) for r in range(ROUND_SLOTS)]
        y_turned = [tile("y_turned%d" % h, [P, W, 4], BF16) for h in range(2)]
        y_codes = [tile("y_codes%d" % h, [P, M], U32) for h in range(2)]
        y_plane = tile("y_plane", [P, 2, M], U8)

        def load_x(a):
            src = x_words.rearrange("g p m t -> p g (m t)")[:, :, 4 * W * a : 4 * W * (a + 1)]
            nc.sync.dma_start(out=x_codes[a][:].bitcast(I32), in_=src.bitcast(I32))

        def load_c(g):
            src = coef_words.rearrange("g p b -> p g b")[:, :, 2 * W * g : 2 * W * (g + 1)]
            nc.sync.dma_start(out=c_raw[:, g].bitcast(I32), in_=src.bitcast(I32))

        def load_scales(plane, scales, cols, quadrants):
            for q in quadrants:
                src = scales.rearrange("g r n -> r g n")[4 * q : 4 * q + 4, :, cols]
                nc.sync.dma_start(out=plane[32 * q : 32 * q + 4].bitcast(I32), in_=src.bitcast(I32))

        def e_rows(g):
            return exposure[W * g : W * (g + 1), :].rearrange("(q t r) n -> t q r n", t=4, r=8)

        def load_e_first(h):
            for t in range(4):
                nc.sync.dma_start(out=e_first[h][:, t, :], in_=e_rows(0)[t][:, :, W * h : W * (h + 1)])

        def load_e(g):
            for t in range(4):
                nc.sync.dma_start(out=e_raw[g][:, t, :], in_=e_rows(g)[t])

        def regroup_c(g0, g1):
            nc.vector.tensor_copy(
                out=c_codes[g0][:].bitcast(I32).rearrange("p t g k (q w) -> p t (g k q) w", w=4),
                in_=c_raw[:, g0:g1].bitcast(I32).rearrange("p g k (q t w) -> p t (g k q) w", t=4, w=4),
            )

        def regroup_c_scales(b, parts):
            for k in range(KG):
                nc.vector.tensor_copy(
                    out=c_plane[b][parts, k].bitcast(I32).rearrange("p t g (q w) -> p t (g q) w", w=2),
                    in_=cs_raw[b][parts, k, :].bitcast(I32).rearrange("p (gq t w) -> p t gq w", t=4, w=2),
                )

        def regroup_severity():
            nc.vector.tensor_copy(
                out=sev_pad[0:FG].rearrange("g t (q r) -> g t q r", r=8),
                in_=sev_row[:].rearrange("g (q t r) -> g t q r", t=4, r=8),
            )

        def turn_severity():
            for t in range(4):
                nc.tensor.transpose(bank[SEV_BANK][:, P * t : P * (t + 1)], sev_pad[:, t, :], ident[:])

        def score(u):
            a, g = divmod(u, FG)
            g0 = max(run[0] for run in C_RUNS if run[0] <= g)
            for t in range(4):
                z = bank[SCORE_BANKS[(4 * u + t) % len(SCORE_BANKS)]]
                for k in range(KG):
                    nc.tensor.matmul_mx(
                        out=z[:],
                        lhsT=c_codes[g0][:, t, g - g0, k, :].bitcast(FP4X4),
                        lhsT_scale=c_plane[g // 2][:, k, t, g % 2, :],
                        rhs=x_codes[a][:, k, :].bitcast(FP8X4),
                        rhs_scale=x_plane[:, k, W * a : W * (a + 1)],
                        start=(k == 0),
                        stop=(k == KG - 1),
                    )
                nc.scalar.activation(out=sig[u % SIG_SLOTS][:, t, :], in_=z[:], func=ACT.Sigmoid)

        def weigh(u):
            g = u % FG
            sev = bank[SEV_BANK][:].rearrange("p (t j) -> p t j", t=4)[:, :, g : g + 1]
            nc.vector.tensor_tensor(
                out=h_bf[:, u % 2].rearrange("p (c i) t -> p c t i", i=2),
                in0=sig[u % SIG_SLOTS][:].rearrange("p t (c i) -> p c t i", i=2),
                in1=sev.unsqueeze(1).broadcast_to([P, W // 2, 4, 2]),
                op=MULT,
            )

        def quant_h(j):
            src = h_bf[:].rearrange("p s m t -> p (s m t)")
            nc.vector.quantize_mx(out=h_codes[j][:].bitcast(FP8X4), scales=h_plane[j][:], in_=src)

        def weave_views(g, h, c0, c1):
            rows = e_first[h][:] if g == 0 else e_raw[g][:, :, W * h : W * (h + 1)]
            return e_bf[:, E_SLOT[(g, h)], c0:c1, :], rows[:, :, c0:c1]

        def weave_by_fours(copy, g, h, c0, c1):
            dst, src = weave_views(g, h, c0, c1)
            copy(out=dst.rearrange("p (c i) t -> p c t i", i=4), in_=src.rearrange("p t (c i) -> p c t i", i=4))

        def weave_gpsimd(g, h, c0, c1):
            dst, src = weave_views(g, h, c0, c1)
            nc.gpsimd.tensor_scalar(
                out=dst, in0=src.rearrange("p t c -> p c t"), scalar1=1.0, scalar2=0.0, op0=MULT, op1=ADD
            )

        def quant_e(c):
            slot = E_SLOT[E_CALLS[c][0]]
            src = e_bf[:, slot : slot + len(E_CALLS[c])].rearrange("p s n t -> p (s n t)")
            nc.vector.quantize_mx(out=e_codes[c][:].bitcast(FP8X4), scales=e_plane[c][:], in_=src)

        def loss(units, groups):
            for v in units:
                i, h = UNITS[v]
                for g in groups:
                    u = FG * (i // 4) + g
                    rows = slice(W * (u % 2) + P * (i % 4), W * (u % 2) + P * (i % 4 + 1))
                    c, j = e_place[(g, h)]
                    cols = slice(W * j, W * (j + 1))
                    nc.tensor.matmul_mx(
                        out=bank[LOSS_BANKS[v % len(LOSS_BANKS)]][:],
                        lhsT=h_codes[u // 2][:, rows].bitcast(FP8X4),
                        lhsT_scale=h_plane[u // 2][:, rows],
                        rhs=e_codes[c][:, cols].bitcast(FP8X4),
                        rhs_scale=e_plane[c][:, cols],
                        start=(g == 0),
                        stop=(g == FG - 1),
                    )

        def log_rows(v, n):
            return sig[(3 + v // 4) % SIG_SLOTS][:, v % 4 : v % 4 + n, :]

        def log1p(*units):
            for v in units:
                src = bank[LOSS_BANKS[v % len(LOSS_BANKS)]]
                nc.scalar.activation(out=log_rows(v, 1)[:, 0, :], in_=src[:], func=ACT.Ln, bias=one[:])

        def y_rows(v, n):
            return y[v // 2 % Y_SLOTS][:, v % 2 : v % 2 + n, :]

        def scale_and_store(k):
            v, n = BATCHES[k]
            i, h = UNITS[v + n - 1]
            cols = slice(W * h, W * (h + 1))
            gain = cap[:, cols].unsqueeze(1).broadcast_to([P, n, W])
            nc.vector.tensor_tensor(out=y_rows(v, n), in0=log_rows(v, n), in1=gain, op=MULT)
            if i % 2 == 1:
                dst = out_0[P * (i - 1) : P * (i + 1), cols].rearrange("(s m) c -> m s c", s=2)
                nc.sync.dma_start(out=dst, in_=y_rows(v + n - 2, 2))

        def round_y(copy, k):
            v, n = BATCHES[k]
            src = y_rows(v, n).rearrange("m s (p u e) -> m u (s p) e", u=2, e=2)
            copy(out=y_bf[k % ROUND_SLOTS][:, :, : P * n, :], in_=src)

        def turn(k):
            pairs = y_bf[k % ROUND_SLOTS][:].rearrange("m u p e -> m u (p e)").bitcast(F32)
            for s in range(BATCHES[k][1]):
                for u in range(2):
                    c = P * (2 * s + u)
                    nc.tensor.transpose(bank[TURN_BANKS[k]][:, c : c + P], pairs[:, u, P * s : P * (s + 1)], ident[:])

        def turned_rows(v, n):
            return y_turned[UNITS[v][1]][:, P * (v % 4) : P * (v % 4 + n), :].rearrange("p m t -> p (m t)")

        def spill(k):
            v, n = BATCHES[k]
            nc.scalar.copy(
                out=turned_rows(v, n).bitcast(F32).rearrange("p (s m u) -> p s m u", s=n, u=2),
                in_=bank[TURN_BANKS[k]][:, : 2 * P * n].rearrange("p (s u m) -> p s m u", s=n, u=2),
            )

        def quant_y(v, n):
            i, h = UNITS[v]
            nc.vector.quantize_mx(
                out=y_codes[h][:, P * i : P * (i + n)].bitcast(FP8X4),
                scales=y_plane[:, h, P * i : P * (i + n)],
                in_=turned_rows(v, n),
            )

        def store_codes(v, n):
            i, h = UNITS[v]
            dst = out_1[h].rearrange("p m t -> p (m t)")[:, 4 * P * i : 4 * P * (i + n)]
            nc.sync.dma_start(out=dst.bitcast(I32), in_=y_codes[h][:, P * i : P * (i + n)].bitcast(I32))

        def store_scales(queues):
            for q, queue in enumerate(queues):
                dst = out_2.rearrange("g r m -> r g m")[4 * q : 4 * q + 4]
                queue.dma_start(out=dst.bitcast(I32), in_=y_plane[32 * q : 32 * q + 4].bitcast(I32))

        on_vector, on_scalar = nc.vector.tensor_copy, nc.scalar.copy
        half = W // 2

        nc.vector.memset(x_plane[:].bitcast(I32), 0)
        nc.vector.memset(large[:], 64.0)
        nc.vector.memset(ident[:], 0.0)
        nc.vector.memset(c_plane[0][:].bitcast(I32), 0)
        nc.vector.memset(cs_raw[1][:].bitcast(I32), 0)
        nc.vector.memset(sev_pad[:], 0.0)
        make_identity(nc, ident[:], nomemset=True)
        nc.scalar.activation(out=one[:], in_=large[:], func=ACT.Sigmoid)
        nc.gpsimd.dma_start(out=sev_row[:], in_=severity.rearrange("(g f) -> g f", g=FG))
        load_scales(cs_raw[0], coef_scales, slice(0, 2 * W), range(4))
        load_scales(x_plane, x_scales, slice(0, M), range(2))
        load_c(0)
        load_x(0)
        load_scales(x_plane, x_scales, slice(0, M), range(2, 4))
        load_e_first(0)
        for g in range(1, FG):
            load_c(g)
        load_scales(cs_raw[1], coef_scales, slice(2 * W, F), range(4))
        load_e_first(1)
        load_e(1)
        load_x(1)
        load_e(2)
        load_e(3)
        nc.sync.dma_start(out=cap[:], in_=capital.partition_broadcast(P))

        for q in range(4):
            regroup_c_scales(0, slice(32 * q, 32 * q + 4))
        regroup_c(*C_RUNS[0])
        regroup_severity()
        score(0)
        turn_severity()
        weave_by_fours(on_vector, 0, 0, 0, W)
        regroup_c(*C_RUNS[1])
        quant_e(0)
        regroup_c(*C_RUNS[2])
        regroup_c_scales(1, slice(0, P))
        for u in range(1, 4):
            score(u)

        weave_by_fours(on_scalar, 1, 1, half, W)
        score(4)
        weave_gpsimd(0, 1, 0, W)
        weigh(0)
        weigh(1)
        quant_h(0)
        quant_e(1)

        weave_by_fours(on_scalar, 2, 1, 0, half)
        score(5)
        loss(range(4), [0])
        weave_gpsimd(1, 0, 0, W)
        weave_gpsimd(1, 1, 0, half)
        weigh(2)
        weigh(3)
        quant_h(1)
        quant_e(2)

        weave_by_fours(on_scalar, 2, 0, half, W)
        score(6)
        loss(range(4), [1])
        weave_by_fours(on_scalar, 2, 1, half, W)
        score(7)
        weave_gpsimd(3, 0, 0, W)
        weave_gpsimd(2, 0, 0, half)
        weigh(4)
        weigh(5)
        quant_e(3)
        quant_h(2)
        quant_e(4)

        loss(range(4), [2, 3])
        loss([4, 5], [0, 1, 2])
        log1p(0, 1, 2, 3)
        loss([6, 7], [0, 1, 2])
        loss([8, 9], [0, 1])
        weave_gpsimd(3, 1, 0, W)
        weigh(6)
        weigh(7)
        quant_e(5)

        loss([4, 5, 6, 7], [3])
        log1p(4, 5)
        scale_and_store(0)
        round_y(on_scalar, 0)
        log1p(6, 7)
        quant_h(3)
        loss([10], [0, 1])
        loss([8], [2, 3])
        turn(0)
        spill(0)
        loss([9, 10], [2, 3])
        log1p(8, 9, 10)
        scale_and_store(1)
        round_y(on_vector, 1)
        turn(1)
        spill(1)
        scale_and_store(2)
        round_y(on_scalar, 2)
        loss([11, 12, 13], range(FG))
        log1p(11, 12, 13)
        turn(2)
        spill(2)
        scale_and_store(3)
        scale_and_store(4)
        round_y(on_vector, 3)
        quant_y(0, 4)
        store_codes(0, 4)
        scale_and_store(5)
        round_y(on_scalar, 5)
        loss([14], range(FG))
        turn(3)
        spill(3)
        loss([15], range(FG))
        log1p(14, 15)
        scale_and_store(6)
        round_y(on_vector, 4)
        turn(4)
        spill(4)
        turn(5)
        spill(5)
        round_y(on_vector, 6)
        quant_y(4, 4)
        store_codes(4, 4)
        scale_and_store(7)
        scale_and_store(8)
        turn(6)
        spill(6)
        round_y(on_vector, 7)
        round_y(on_vector, 8)
        for k in (7, 8):
            turn(k)
            spill(k)
        quant_y(8, 4)
        store_codes(8, 4)
        quant_y(12, 2)
        quant_y(14, 1)
        store_codes(12, 3)
        quant_y(15, 1)
        store_codes(15, 1)
        store_scales([nc.sync, nc.scalar, nc.sync, nc.scalar])
